import numpy as np
import ml_dtypes


def mxq(x, axis, fmt="e4m3"):
    dtype, down = {"e4m3": (ml_dtypes.float8_e4m3fn, 7), "e5m2": (ml_dtypes.float8_e5m2, 14)}[fmt]
    v = np.moveaxis(np.asarray(x, np.float32).astype(ml_dtypes.bfloat16).astype(np.float64), axis, -1)
    blocks = v.reshape(v.shape[:-1] + (-1, 32))
    amax = np.abs(blocks).max(-1, keepdims=True)
    byte = np.maximum(np.where(amax > 0, np.frexp(amax)[1] - 1 + 127, 0) - down, 1)
    scale = np.exp2(byte - 127.0)
    codes = (blocks / scale).astype(np.float32).astype(dtype).astype(np.float64)
    return np.moveaxis((codes * scale).reshape(v.shape), -1, axis)


WIDE = False


def mx_kscale(k):
    if not WIDE:
        return np.ones(k)
    levels = np.array([10, -10, 5, -5, 0])
    if k % 512:
        return np.exp2(np.random.permutation(np.resize(levels, k // 32))).repeat(32)
    a = np.empty((k // 512, 16))
    for p in range(k // 512):
        a[p, :8] = np.random.permutation(np.resize(levels, 8))
        for g in range(8):
            far = levels[np.abs(levels - a[p, g]) >= 10]
            a[p, g + 8] = far[np.random.randint(len(far))]
    return np.exp2(a.ravel()).repeat(32)


def f64(x):
    return np.asarray(x).astype(np.float64)


def striped(idx):
    return np.tile(idx.reshape(-1, 16).T, (8, 1)).astype(np.uint16)


def unstriped(offs):
    return offs[:16].T.reshape(-1).astype(np.int64)


E2M1 = np.array([0.0, 0.5, 1.0, 1.5, 2.0, 3.0, 4.0, 6.0, -0.0, -0.5, -1.0, -1.5, -2.0, -3.0, -4.0, -6.0])


def pack_weight(w, fmt):
    k, n = w.shape
    w = f64(np.asarray(w, np.float32).astype(ml_dtypes.bfloat16)).reshape(k // 32, 32, n)
    amax = np.abs(w).max(1)
    if fmt == "e4m3":
        byte = np.frexp(amax)[1] - 1 + 127 - 7
    else:
        mant, ex = np.frexp(amax / 6.0)
        byte = np.where(mant > 0.5, ex, ex - 1) + 127
    byte = np.clip(np.where(amax > 0, byte, 1), 1, 254)
    scaled = (w * np.exp2(127.0 - byte)[:, None, :]).reshape(k, n).astype(np.float32)
    by_word = np.ascontiguousarray(scaled.reshape(k // 512, 128, 4, n).transpose(0, 1, 3, 2))
    if fmt == "e4m3":
        words = by_word.astype(ml_dtypes.float8_e4m3fn).view(np.uint8)
    else:
        c = by_word.astype(ml_dtypes.float4_e2m1fn).view(np.uint8) & 0xF
        words = (c[..., 0::2] | (c[..., 1::2] << 4)).reshape(k // 512, 128, 2 * n)
    return np.ascontiguousarray(words), np.ascontiguousarray(byte.astype(np.uint8).reshape(k // 512, 16, n))


def unpack_weight(words, scales, fmt):
    g, _, n = scales.shape
    words = np.ascontiguousarray(words).reshape(g, 128, n, -1)
    if fmt == "e4m3":
        vals = words.view(ml_dtypes.float8_e4m3fn).astype(np.float64)
    else:
        nib = np.empty((g, 128, n, 4), np.uint8)
        nib[..., 0::2] = words & 0xF
        nib[..., 1::2] = words >> 4
        vals = E2M1[nib]
    vals = vals * np.repeat(np.exp2(scales.astype(np.float64) - 127.0), 8, axis=1)[..., None]
    return vals.transpose(0, 1, 3, 2).reshape(g * 512, n)


def relu(v):
    return np.maximum(v, 0.0)


K, T, E, C, H, HS, N = 1024, 512, 8, 128, 512, 1024, 256


def by_expert(wq, xq):
    return np.concatenate([wq[e].T @ xq[:, e * C:(e + 1) * C] for e in range(E)], axis=1)


def setup_inputs():
    n = np.random.standard_normal
    s = mx_kscale(K)
    u = mx_kscale(H)
    v = mx_kscale(HS)
    first = np.random.permutation(np.repeat(np.arange(E), T // E))
    second = (first + 1 + np.random.permutation(np.repeat(np.arange(E - 1), -(-T // (E - 1)))[:T])) % E
    while np.bincount(second, minlength=E).max() != T // E:
        load = np.bincount(second, minlength=E); hi, lo = int(load.argmax()), int(load.argmin())
        t = np.flatnonzero((second == hi) & (first != lo))[0]; second[t] = lo
    slot_token = np.empty(E * C, np.int64); pos = np.empty((2, T), np.int64); fill = np.zeros(E, np.int64)
    place = np.stack([np.random.permutation(C) for _ in range(E)])
    for r, deal in enumerate((first, second)):
        for t in np.random.permutation(T):
            e = deal[t]; j = e * C + place[e, fill[e]]; fill[e] += 1; slot_token[j] = t; pos[r, t] = j
    g = np.random.uniform(0.2, 0.8, T)
    x = pack_weight(n((K, T)) * s[:, None], "e4m3")
    w1 = [pack_weight(m, "e2m1") for m in n((E, K, H)) / np.sqrt(K) / s[None, :, None] * u]
    w2 = [pack_weight(m, "e2m1") for m in n((E, H, N)) / np.sqrt(H) / u[None, :, None]]
    w1s = pack_weight(n((K, HS)) / np.sqrt(K) / s[:, None] * v, "e4m3")
    w2s = pack_weight(n((HS, N)) / np.sqrt(HS) / v[:, None], "e4m3")
    return {
        "x_words": x[0],
        "x_scales": x[1],
        "w1_words": np.stack([m[0] for m in w1]),
        "w1_scales": np.stack([m[1] for m in w1]),
        "w2_words": np.stack([m[0] for m in w2]),
        "w2_scales": np.stack([m[1] for m in w2]),
        "w1s_words": w1s[0],
        "w1s_scales": w1s[1],
        "w2s_words": w2s[0],
        "w2s_scales": w2s[1],
        "gate": np.stack([np.tile(g, (128, 1)), np.tile(1.0 - g, (128, 1))]).astype(np.float32),
        "offs": striped(slot_token),
        "pos1": striped(pos[0]),
        "pos2": striped(pos[1]),
    }


def reference(x_words, x_scales, w1_words, w1_scales, w2_words, w2_scales, w1s_words, w1s_scales, w2s_words, w2s_scales, gate, offs, pos1, pos2):
    w1 = np.stack([unpack_weight(w1_words[e], w1_scales[e], "e2m1") for e in range(E)])
    w2 = np.stack([unpack_weight(w2_words[e], w2_scales[e], "e2m1") for e in range(E)])
    w1s = unpack_weight(w1s_words, w1s_scales, "e4m3")
    w2s = unpack_weight(w2s_words, w2s_scales, "e4m3")
    idx = unstriped(offs)
    x = unpack_weight(x_words, x_scales, "e4m3")
    hs = relu(w1s.T @ x)
    ys = w2s.T @ mxq(hs, 0, "e4m3")
    h = relu(by_expert(w1, x[:, idx]))
    y = by_expert(w2, mxq(h, 0, "e4m3"))
    c = sum(f64(gate[r, :1]) * y[:, unstriped(p)] for r, p in enumerate((pos1, pos2)))
    return ys + c

@@ -1,0 +1,198 @@
+from contextlib import ExitStack
+
+import concourse.mybir as mybir
+from concourse.masks import make_identity
+
+K, T, E, C, H, HS, N = 1024, 512, 8, 128, 512, 1024, 256
+FLOPS = 2 * (T * (K * HS + HS * N) + E * C * (K * H + H * N))
+
+F32 = mybir.dt.float32
+BF16 = mybir.dt.bfloat16
+I32 = mybir.dt.int32
+U32 = mybir.dt.uint32
+U16 = mybir.dt.uint16
+U8 = mybir.dt.uint8
+FP8X4 = mybir.dt.float8_e4m3fn_x4
+FP4X4 = mybir.dt.float4_e2m1fn_x4
+RELU = mybir.ActivationFunctionType.Relu
+MULT = mybir.AluOpType.mult
+ADD = mybir.AluOpType.add
+
+P = 128
+PASSES = K // 512
+SLOTS = E * C
+PAIRS = E // 2
+GATHER_RUNS = [(0, 1), (1, 2), (2, 4), (4, 6), (6, 7), (7, 8)]
+
+
+def tile_moe_shf_mlp_relu_kernel(
+    tc, x_words, x_scales, w1_words, w1_scales, w2_words, w2_scales, w1s_words, w1s_scales, w2s_words, w2s_scales, gate, offs, pos1, pos2, out
+):
+    nc = tc.nc
+    with ExitStack() as ctx:
+        keep = ctx.enter_context(tc.tile_pool(name="keep", bufs=1))
+        ring = ctx.enter_context(tc.tile_pool(name="ring", bufs=4))
+        psum = ctx.enter_context(tc.psum_pool(name="psum", bufs=1))
+
+        def held(shape, dtype, name):
+            return keep.tile(shape, dtype, name=name, align_bytes=64)
+
+        def zeroed_plane(shape, name):
+            plane = held(shape, U8, name)
+            nc.vector.memset(plane[:].bitcast(I32), 0)
+            return plane
+
+        def load_rows(plane, rows):
+            for r in range(4):
+                nc.sync.dma_start(out=plane[:].bitcast(I32)[r:P:32], in_=rows[r].bitcast(I32))
+
+        def load_packed(plane, scales, first):
+            for q in range(4):
+                nc.sync.dma_start(
+                    out=plane[:].bitcast(I32)[32 * q + first : 32 * q + first + 8], in_=scales[:, 4 * q : 4 * q + 4, :].bitcast(I32)
+                )
+
+        x_plane = zeroed_plane([P, PASSES, T], "x_plane")
+        w1_plane = [zeroed_plane([P, 4 * PASSES, H], f"w1_plane{h}") for h in range(2)]
+        w2_plane = zeroed_plane([P, E, N], "w2_plane")
+        w1s_plane = zeroed_plane([P, HS], "w1s_plane")
+        w2s_plane = zeroed_plane([P, N], "w2s_plane")
+        ident = held([P, P], F32, "ident")
+        make_identity(nc, ident[:])
+
+        slot_list = keep.tile([P, SLOTS // 16], U16, name="slot_list")
+        nc.sync.dma_start(slot_list[:], offs)
+        x_sb = [held([P, T], I32, f"x_sb{s}") for s in range(PASSES)]
+        for s in range(PASSES):
+            nc.sync.dma_start(out=x_sb[s][:], in_=x_words[s].rearrange("p t d -> p (t d)").bitcast(I32))
+        load_rows(x_plane, x_scales.rearrange("s (q r) t -> r q s t", r=4))
+
+        w1_sb = [held([P, 2 * PASSES, 2 * H], U8, f"w1_sb{i}") for i in range(PAIRS)]
+
+        def load_w1(i):
+            nc.sync.dma_start(out=w1_sb[i][:].bitcast(I32), in_=w1_words[2 * i : 2 * i + 2].rearrange("e s p b -> p (e s) b").bitcast(I32))
+
+        def load_w1_plane(h):
+            load_rows(w1_plane[h], w1_scales[4 * h : 4 * h + 4].rearrange("e s (q r) i -> r q (e s) i", r=4))
+
+        load_w1(0)
+        load_w1_plane(0)
+        load_w1(1)
+        load_w1_plane(1)
+        load_w1(2)
+        load_w1(3)
+        w2_sb = held([P, E, 2 * N], U8, "w2_sb")
+        nc.sync.dma_start(out=w2_sb[:].bitcast(I32), in_=w2_words.rearrange("e s p b -> p (e s) b").bitcast(I32))
+        load_rows(w2_plane, w2_scales.rearrange("e s (q r) n -> r q (e s) n", r=4))
+        w1s_sb = [held([P, PASSES, 512], I32, f"w1s_sb{g}") for g in range(2)]
+        w1s_rows = w1s_words.rearrange("s p l d -> p s (l d)").bitcast(I32)
+        nc.sync.dma_start(out=w1s_sb[0][:], in_=w1s_rows[:, :, 0:512])
+        load_packed(w1s_plane, w1s_scales, 4)
+        nc.sync.dma_start(out=w1s_sb[1][:], in_=w1s_rows[:, :, 512:1024])
+        token_lists = [keep.tile([P, T // 16], U16, name=f"token_list{r}") for r in range(2)]
+        nc.sync.dma_start(token_lists[0][:], pos1)
+        nc.sync.dma_start(token_lists[1][:], pos2)
+        gate_sb = held([P, 2, T], F32, "gate_sb")
+        nc.sync.dma_start(out=gate_sb[:], in_=gate.rearrange("r p t -> p r t"))
+        w2s_sb = held([P, 2, N], I32, "w2s_sb")
+        nc.sync.dma_start(out=w2s_sb[:], in_=w2s_words.rearrange("s p n d -> p s (n d)").bitcast(I32))
+        load_packed(w2s_plane, w2s_scales, 8)
+
+        picked = {}
+        for lo, hi in GATHER_RUNS:
+            n = (hi - lo) * C
+            offsets = slot_list[:, lo * C // 16 : hi * C // 16]
+            words = [held([P, n], U32, f"words{lo}_{s}") for s in range(PASSES)]
+            scales = [held([P, n], U8, f"scales{lo}_{s}") for s in range(PASSES)]
+            for s in range(PASSES):
+                nc.vector.tensor_copy(words[s][:], x_sb[s][:].bitcast(U32).indirect(offsets))
+                nc.vector.tensor_copy(scales[s][:], x_plane[:, s, :].indirect(offsets))
+            for e in range(lo, hi):
+                cols = slice((e - lo) * C, (e - lo + 1) * C)
+                picked[e] = [(words[s][:, cols], scales[s][:, cols]) for s in range(PASSES)]
+
+        def first_layer(tokens, weights):
+            acc = psum.tile([P, 512], F32, name="acc", bufs=4)
+            for s in range(PASSES):
+                nc.tensor.matmul_mx(
+                    out=acc[:], lhsT=tokens[s][0].bitcast(FP8X4), lhsT_scale=tokens[s][1],
+                    rhs=weights[s][0], rhs_scale=weights[s][1], start=(s == 0), stop=(s == PASSES - 1),
+                )
+            hidden = ring.tile([P, 512], BF16, name="hidden")
+            nc.scalar.activation(
+                out=hidden[:].rearrange("s (u p e) -> s u p e", u=2, e=2), in_=acc[:].rearrange("s (p u e) -> s u p e", u=2, e=2), func=RELU
+            )
+            return hidden
+
+        def turn(hiddens):
+            turned = psum.tile([P, 2, 2, P], F32, name="turned", bufs=2)
+            for j, hidden in enumerate(hiddens):
+                for u in range(2):
+                    nc.tensor.transpose(turned[:, j, u, :], hidden[:].bitcast(F32)[:, u * P : (u + 1) * P], ident[:])
+            grouped = ring.tile([P, 2 * P * 4], BF16, name="grouped", align_bytes=64)
+            nc.scalar.copy(
+                out=grouped[:].bitcast(F32).rearrange("p (j s u) -> p j s u", j=2, u=2), in_=turned[:].rearrange("p j u s -> p j s u")
+            )
+            return grouped
+
+        def quantise(grouped, name):
+            codes = held([P, 2 * P], U32, f"codes_{name}")
+            plane = held([P, 2 * P], U8, f"plane_{name}")
+            nc.vector.quantize_mx(out=codes[:].bitcast(FP8X4), scales=plane[:], in_=grouped[:])
+            return codes, plane
+
+        y_sb = [held([P, SLOTS], F32, f"y_sb{b}") for b in range(2)]
+
+        for i in range(PAIRS):
+            hiddens = []
+            for e in (2 * i, 2 * i + 1):
+                weights = [
+                    (w1_sb[i][:, (e % 2) * PASSES + s, :].bitcast(FP4X4), w1_plane[e // 4][:, (e % 4) * PASSES + s, :]) for s in range(PASSES)
+                ]
+                hiddens.append(first_layer(picked[e], weights))
+            codes, plane = quantise(turn(hiddens), f"h{i}")
+            res = psum.tile([P, 2, 2 * C], F32, name="res", bufs=2)
+            for b in range(2):
+                for j in range(2):
+                    e = 2 * i + j
+                    nc.tensor.matmul_mx(
+                        out=res[:, b, j * C : (j + 1) * C],
+                        lhsT=w2_sb[:, e, b * 256 : (b + 1) * 256].bitcast(FP4X4), lhsT_scale=w2_plane[:, e, b * P : (b + 1) * P],
+                        rhs=codes[:, j * C : (j + 1) * C].bitcast(FP8X4), rhs_scale=plane[:, j * C : (j + 1) * C], start=True, stop=True,
+                    )
+            cols = slice(2 * i * C, (2 * i + 2) * C)
+            nc.vector.tensor_copy(y_sb[0][:, cols], res[:, 0, :])
+            if i < PAIRS - 1:
+                nc.vector.tensor_copy(y_sb[1][:, cols], res[:, 1, :])
+            else:
+                nc.scalar.copy(y_sb[1][:, cols], res[:, 1, :])
+
+        out_rows = out.rearrange("(b p) t -> p b t", p=P)
+        for half in range(2):
+            made = []
+            for g in range(2):
+                weights = [(w1s_sb[g][:, s, :].bitcast(FP8X4), w1s_plane[4 + 4 * s :, g * 512 : (g + 1) * 512]) for s in range(PASSES)]
+                hiddens = []
+                for j in range(2):
+                    cols = slice((2 * half + j) * P, (2 * half + j + 1) * P)
+                    hiddens.append(first_layer([(x_sb[s][:, cols], x_plane[:, s, cols]) for s in range(PASSES)], weights))
+                made.append(quantise(turn(hiddens), f"hs{half}_{g}"))
+            res = psum.tile([P, 2, 2 * C], F32, name="res", bufs=2)
+            for b in range(2):
+                for g in range(2):
+                    nc.tensor.matmul_mx(
+                        out=res[:, b, :],
+                        lhsT=w2s_sb[:, g, b * P : (b + 1) * P].bitcast(FP8X4), lhsT_scale=w2s_plane[8 + 4 * g :, b * P : (b + 1) * P],
+                        rhs=made[g][0][:].bitcast(FP8X4), rhs_scale=made[g][1][:], start=(g == 0), stop=(g == 1),
+                    )
+            tokens = slice(half * 256, (half + 1) * 256)
+            terms = [held([P, 2, 256], F32, f"term{half}_{r}") for r in range(2)]
+            for r in range(2):
+                offsets = token_lists[r][:, half * 16 : (half + 1) * 16]
+                for b in range(2):
+                    nc.vector.tensor_tensor(terms[r][:, b, :], y_sb[b][:].indirect(offsets), gate_sb[:, r, tokens], MULT)
+            routed = held([P, 2, 256], F32, f"routed{half}")
+            nc.vector.tensor_tensor(routed[:], terms[0][:], terms[1][:], ADD)
+            total = held([P, 2, 256], F32, f"total{half}")
+            nc.vector.tensor_tensor(total[:], res[:], routed[:], ADD)
+            nc.sync.dma_start(out=out_rows[:, :, tokens], in_=total[:])

@@ -21,8 +21,14 @@ ADD = mybir.AluOpType.add
 P = 128
 PASSES = K // 512
 SLOTS = E * C
-PAIRS = E // 2
-GATHER_RUNS = [(0, 1), (1, 2), (2, 4), (4, 6), (6, 7), (7, 8)]
+GATHER_RUNS = [(0, 2), (2, 4), (4, 6), (6, 7), (7, 8)]
+GROUPS = [(0, 2), (2, 4), (4, 6), (6, 7), (7, 8)]
+SUM_BANKS = [0, 1, 2, 0, 1, 2, 0, 2]
+TURN_BANKS = [3, 4, 5, 6, 7]
+SHARED_BANKS = [2, 0, 1]
+AHEAD = 1
+YS_BANKS = [2, 0]
+RESULT_BANKS = [1, 4, 5, 6, 7]
 
 
 def tile_moe_shf_mlp_relu_kernel(
@@ -31,19 +37,18 @@ def tile_moe_shf_mlp_relu_kernel(
     nc = tc.nc
     with ExitStack() as ctx:
         keep = ctx.enter_context(tc.tile_pool(name="keep", bufs=1))
-        ring = ctx.enter_context(tc.tile_pool(name="ring", bufs=4))
         psum = ctx.enter_context(tc.psum_pool(name="psum", bufs=1))
 
         def held(shape, dtype, name):
             return keep.tile(shape, dtype, name=name, align_bytes=64)
 
-        def zeroed_plane(shape, name):
+        def zeroed_plane(shape, name, engine):
             plane = held(shape, U8, name)
-            nc.vector.memset(plane[:].bitcast(I32), 0)
+            engine.memset(plane[:].bitcast(I32), 0)
             return plane
 
-        def load_rows(plane, rows):
-            for r in range(4):
+        def load_rows(plane, rows, which):
+            for r in which:
                 nc.sync.dma_start(out=plane[:].bitcast(I32)[r:P:32], in_=rows[r].bitcast(I32))
 
         def load_packed(plane, scales, first):
@@ -52,49 +57,44 @@ def tile_moe_shf_mlp_relu_kernel(
                     out=plane[:].bitcast(I32)[32 * q + first : 32 * q + first + 8], in_=scales[:, 4 * q : 4 * q + 4, :].bitcast(I32)
                 )
 
-        x_plane = zeroed_plane([P, PASSES, T], "x_plane")
-        w1_plane = [zeroed_plane([P, 4 * PASSES, H], f"w1_plane{h}") for h in range(2)]
-        w2_plane = zeroed_plane([P, E, N], "w2_plane")
-        w1s_plane = zeroed_plane([P, HS], "w1s_plane")
-        w2s_plane = zeroed_plane([P, N], "w2s_plane")
+        x_plane = zeroed_plane([P, PASSES, T], "x_plane", nc.gpsimd)
+        w1_plane = [zeroed_plane([P, 4 * PASSES, H], f"w1_plane{h}", nc.vector) for h in range(2)]
+        w2_plane = zeroed_plane([P, E, N], "w2_plane", nc.vector)
+        w1s_plane = zeroed_plane([P, HS], "w1s_plane", nc.vector)
+        w2s_plane = zeroed_plane([P, N], "w2s_plane", nc.vector)
         ident = held([P, P], F32, "ident")
         make_identity(nc, ident[:])
 
+        x_sb = held([P, PASSES, T], I32, "x_sb")
+        nc.sync.dma_start(out=x_sb[:], in_=x_words.rearrange("s p t d -> p s (t d)").bitcast(I32))
+        load_rows(x_plane, x_scales.rearrange("s (q r) t -> r q s t", r=4), range(4))
         slot_list = keep.tile([P, SLOTS // 16], U16, name="slot_list")
         nc.sync.dma_start(slot_list[:], offs)
-        x_sb = [held([P, T], I32, f"x_sb{s}") for s in range(PASSES)]
-        for s in range(PASSES):
-            nc.sync.dma_start(out=x_sb[s][:], in_=x_words[s].rearrange("p t d -> p (t d)").bitcast(I32))
-        load_rows(x_plane, x_scales.rearrange("s (q r) t -> r q s t", r=4))
-
-        w1_sb = [held([P, 2 * PASSES, 2 * H], U8, f"w1_sb{i}") for i in range(PAIRS)]
+        w1_sb = [held([P, 2 * PASSES, 2 * H], U8, f"w1_sb{i}") for i in range(E // 2)]
 
         def load_w1(i):
             nc.sync.dma_start(out=w1_sb[i][:].bitcast(I32), in_=w1_words[2 * i : 2 * i + 2].rearrange("e s p b -> p (e s) b").bitcast(I32))
 
-        def load_w1_plane(h):
-            load_rows(w1_plane[h], w1_scales[4 * h : 4 * h + 4].rearrange("e s (q r) i -> r q (e s) i", r=4))
-
-        load_w1(0)
-        load_w1_plane(0)
-        load_w1(1)
-        load_w1_plane(1)
-        load_w1(2)
-        load_w1(3)
         w2_sb = held([P, E, 2 * N], U8, "w2_sb")
-        nc.sync.dma_start(out=w2_sb[:].bitcast(I32), in_=w2_words.rearrange("e s p b -> p (e s) b").bitcast(I32))
-        load_rows(w2_plane, w2_scales.rearrange("e s (q r) n -> r q (e s) n", r=4))
         w1s_sb = [held([P, PASSES, 512], I32, f"w1s_sb{g}") for g in range(2)]
         w1s_rows = w1s_words.rearrange("s p l d -> p s (l d)").bitcast(I32)
-        nc.sync.dma_start(out=w1s_sb[0][:], in_=w1s_rows[:, :, 0:512])
-        load_packed(w1s_plane, w1s_scales, 4)
-        nc.sync.dma_start(out=w1s_sb[1][:], in_=w1s_rows[:, :, 512:1024])
         token_lists = [keep.tile([P, T // 16], U16, name=f"token_list{r}") for r in range(2)]
+        gate_sb = held([P, 2, T], F32, "gate_sb")
+        w2s_sb = held([P, 2, N], I32, "w2s_sb")
+        load_w1(0)
+        load_rows(w1_plane[0], w1_scales[0 : 4].rearrange("e s (q r) i -> r q (e s) i", r=4), range(4))
+        load_w1(1)
+        load_rows(w1_plane[1], w1_scales[4 : 8].rearrange("e s (q r) i -> r q (e s) i", r=4), range(4))
+        load_w1(2)
+        load_rows(w2_plane, w2_scales.rearrange("e s (q r) n -> r q (e s) n", r=4), range(0, 4))
+        load_packed(w1s_plane, w1s_scales, 4)
         nc.sync.dma_start(token_lists[0][:], pos1)
         nc.sync.dma_start(token_lists[1][:], pos2)
-        gate_sb = held([P, 2, T], F32, "gate_sb")
+        load_w1(3)
+        nc.sync.dma_start(out=w2_sb[:].bitcast(I32), in_=w2_words.rearrange("e s p b -> p (e s) b").bitcast(I32))
+        nc.sync.dma_start(out=w1s_sb[0][:], in_=w1s_rows[:, :, 0:512])
         nc.sync.dma_start(out=gate_sb[:], in_=gate.rearrange("r p t -> p r t"))
-        w2s_sb = held([P, 2, N], I32, "w2s_sb")
+        nc.sync.dma_start(out=w1s_sb[1][:], in_=w1s_rows[:, :, 512:1024])
         nc.sync.dma_start(out=w2s_sb[:], in_=w2s_words.rearrange("s p n d -> p s (n d)").bitcast(I32))
         load_packed(w2s_plane, w2s_scales, 8)
 
@@ -105,94 +105,125 @@ def tile_moe_shf_mlp_relu_kernel(
             words = [held([P, n], U32, f"words{lo}_{s}") for s in range(PASSES)]
             scales = [held([P, n], U8, f"scales{lo}_{s}") for s in range(PASSES)]
             for s in range(PASSES):
-                nc.vector.tensor_copy(words[s][:], x_sb[s][:].bitcast(U32).indirect(offsets))
+                nc.vector.tensor_copy(words[s][:], x_sb[:, s, :].bitcast(U32).indirect(offsets))
                 nc.vector.tensor_copy(scales[s][:], x_plane[:, s, :].indirect(offsets))
             for e in range(lo, hi):
                 cols = slice((e - lo) * C, (e - lo + 1) * C)
                 picked[e] = [(words[s][:, cols], scales[s][:, cols]) for s in range(PASSES)]
 
-        def first_layer(tokens, weights):
-            acc = psum.tile([P, 512], F32, name="acc", bufs=4)
+        banks = [psum.tile([P, 512], F32, name=f"bank{b}") for b in range(8)]
+
+        def first_layer(acc, tokens, weights, hidden):
             for s in range(PASSES):
                 nc.tensor.matmul_mx(
                     out=acc[:], lhsT=tokens[s][0].bitcast(FP8X4), lhsT_scale=tokens[s][1],
                     rhs=weights[s][0], rhs_scale=weights[s][1], start=(s == 0), stop=(s == PASSES - 1),
                 )
-            hidden = ring.tile([P, 512], BF16, name="hidden")
             nc.scalar.activation(
-                out=hidden[:].rearrange("s (u p e) -> s u p e", u=2, e=2), in_=acc[:].rearrange("s (p u e) -> s u p e", u=2, e=2), func=RELU
+                out=hidden.bitcast(BF16).rearrange("s (u p e) -> s u p e", u=2, e=2), in_=acc[:].rearrange("s (p u e) -> s u p e", u=2, e=2), func=RELU
             )
             return hidden
 
-        def turn(hiddens):
-            turned = psum.tile([P, 2, 2, P], F32, name="turned", bufs=2)
-            for j, hidden in enumerate(hiddens):
+        def turn_and_quantise(bank, hiddens, grouped, name):
+            count = len(hiddens)
+            turned = bank[:, 0 : count * 256].rearrange("p (j u s) -> p j u s", j=count, u=2)
+            for j in reversed(range(count)):
                 for u in range(2):
-                    nc.tensor.transpose(turned[:, j, u, :], hidden[:].bitcast(F32)[:, u * P : (u + 1) * P], ident[:])
-            grouped = ring.tile([P, 2 * P * 4], BF16, name="grouped", align_bytes=64)
-            nc.scalar.copy(
-                out=grouped[:].bitcast(F32).rearrange("p (j s u) -> p j s u", j=2, u=2), in_=turned[:].rearrange("p j u s -> p j s u")
-            )
-            return grouped
-
-        def quantise(grouped, name):
-            codes = held([P, 2 * P], U32, f"codes_{name}")
-            plane = held([P, 2 * P], U8, f"plane_{name}")
-            nc.vector.quantize_mx(out=codes[:].bitcast(FP8X4), scales=plane[:], in_=grouped[:])
+                    nc.tensor.transpose(turned[:, j, u, :], hiddens[j][:, u * P : (u + 1) * P], ident[:])
+            nc.scalar.copy(out=grouped.rearrange("p (j s u) -> p j s u", j=count, u=2), in_=turned.rearrange("p j u s -> p j s u"))
+            codes = held([P, count * P], U32, f"codes_{name}")
+            plane = held([P, count * P], U8, f"plane_{name}")
+            nc.vector.quantize_mx(out=codes[:].bitcast(FP8X4), scales=plane[:], in_=grouped.bitcast(BF16))
             return codes, plane
+
+        def routed_hidden(e):
+            weights = [(w1_sb[e // 2][:, (e % 2) * PASSES + s, :].bitcast(FP4X4), w1_plane[e // 4][:, (e % 4) * PASSES + s, :]) for s in range(PASSES)]
+            return first_layer(banks[SUM_BANKS[e]], picked[e], weights, held([P, 256], F32, f"hidden{e}")[:])
 
         y_sb = [held([P, SLOTS], F32, f"y_sb{b}") for b in range(2)]
 
-        for i in range(PAIRS):
-            hiddens = []
-            for e in (2 * i, 2 * i + 1):
-                weights = [
-                    (w1_sb[i][:, (e % 2) * PASSES + s, :].bitcast(FP4X4), w1_plane[e // 4][:, (e % 4) * PASSES + s, :]) for s in range(PASSES)
-                ]
-                hiddens.append(first_layer(picked[e], weights))
-            codes, plane = quantise(turn(hiddens), f"h{i}")
-            res = psum.tile([P, 2, 2 * C], F32, name="res", bufs=2)
+        def routed_results(group, codes, plane):
+            lo, hi = GROUPS[group]
+            bank = banks[RESULT_BANKS[group]]
             for b in range(2):
-                for j in range(2):
-                    e = 2 * i + j
+                for e in range(lo, hi):
+                    j = e - lo
                     nc.tensor.matmul_mx(
-                        out=res[:, b, j * C : (j + 1) * C],
+                        out=bank[:, b * 256 + j * C : b * 256 + (j + 1) * C],
                         lhsT=w2_sb[:, e, b * 256 : (b + 1) * 256].bitcast(FP4X4), lhsT_scale=w2_plane[:, e, b * P : (b + 1) * P],
                         rhs=codes[:, j * C : (j + 1) * C].bitcast(FP8X4), rhs_scale=plane[:, j * C : (j + 1) * C], start=True, stop=True,
                     )
-            cols = slice(2 * i * C, (2 * i + 2) * C)
-            nc.vector.tensor_copy(y_sb[0][:, cols], res[:, 0, :])
-            if i < PAIRS - 1:
-                nc.vector.tensor_copy(y_sb[1][:, cols], res[:, 1, :])
-            else:
-                nc.scalar.copy(y_sb[1][:, cols], res[:, 1, :])
+            for b in range(2):
+                copy = nc.scalar.copy if (group, b) in [] else nc.vector.tensor_copy
+                copy(y_sb[b][:, lo * C : hi * C], bank[:, b * 256 : b * 256 + (hi - lo) * C])
+
+        hiddens, made = {}, {}
+
+        def routed_sums(group):
+            for e in range(*GROUPS[group]):
+                hiddens[e] = routed_hidden(e)
+
+        def routed_codes(group):
+            lo, hi = GROUPS[group]
+            grouped = held([P, (hi - lo) * 256], F32, f"grouped{group}")
+            made[group] = turn_and_quantise(banks[TURN_BANKS[group]], [hiddens[e] for e in range(lo, hi)], grouped[:], f"h{group}")
+
+        routed_sums(0)
+        routed_sums(1)
+        routed_codes(0)
+        routed_sums(2)
+        routed_codes(1)
+        routed_sums(3)
+        routed_codes(2)
+        routed_sums(4)
+        routed_codes(3)
+        routed_codes(4)
+        routed_results(0, *made[0])
+        routed_results(1, *made[1])
+        routed_results(2, *made[2])
+        routed_results(3, *made[3])
+        routed_results(4, *made[4])
+
+        slots = [held([P, 256], F32, f"slot{k}") for k in range(3)]
+        last = held([P, 512], F32, "last")
+
+        def shared_hidden(unit):
+            g, half, j = unit // 4, unit // 2 % 2, unit % 2
+            weights = [(w1s_sb[g][:, s, :].bitcast(FP8X4), w1s_plane[4 + 4 * s :, g * 512 : (g + 1) * 512]) for s in range(PASSES)]
+            cols = slice((2 * half + j) * P, (2 * half + j + 1) * P)
+            return first_layer(banks[SHARED_BANKS[unit % len(SHARED_BANKS)]], [(x_sb[:, s, cols], x_plane[:, s, cols]) for s in range(PASSES)], weights, slots[unit // 2 - 1][:] if j == 1 and unit > 1 else held([P, 256], F32, f"shared{unit}")[:])
+
+        shared = []
+        units = []
+        for pair in range(4):
+            units.extend(shared_hidden(unit) for unit in range(len(units), min(2 * pair + 2 + AHEAD, 8)))
+            shared.append(turn_and_quantise(banks[3 + pair % 2], units[2 * pair : 2 * pair + 2], last[:] if pair == 3 else held([P, 512], F32, f"grouped_s{pair}")[:], f"hs{pair}"))
 
         out_rows = out.rearrange("(b p) t -> p b t", p=P)
         for half in range(2):
-            made = []
-            for g in range(2):
-                weights = [(w1s_sb[g][:, s, :].bitcast(FP8X4), w1s_plane[4 + 4 * s :, g * 512 : (g + 1) * 512]) for s in range(PASSES)]
-                hiddens = []
-                for j in range(2):
-                    cols = slice((2 * half + j) * P, (2 * half + j + 1) * P)
-                    hiddens.append(first_layer([(x_sb[s][:, cols], x_plane[:, s, cols]) for s in range(PASSES)], weights))
-                made.append(quantise(turn(hiddens), f"hs{half}_{g}"))
-            res = psum.tile([P, 2, 2 * C], F32, name="res", bufs=2)
+            bank = banks[YS_BANKS[half]]
             for b in range(2):
                 for g in range(2):
+                    codes, plane = shared[2 * g + half]
                     nc.tensor.matmul_mx(
-                        out=res[:, b, :],
+                        out=bank[:, b * 256 : (b + 1) * 256],
                         lhsT=w2s_sb[:, g, b * P : (b + 1) * P].bitcast(FP8X4), lhsT_scale=w2s_plane[8 + 4 * g :, b * P : (b + 1) * P],
-                        rhs=made[g][0][:].bitcast(FP8X4), rhs_scale=made[g][1][:], start=(g == 0), stop=(g == 1),
+                        rhs=codes[:].bitcast(FP8X4), rhs_scale=plane[:], start=(g == 0), stop=(g == 1),
                     )
             tokens = slice(half * 256, (half + 1) * 256)
-            terms = [held([P, 2, 256], F32, f"term{half}_{r}") for r in range(2)]
+            pieces = {}
             for r in range(2):
                 offsets = token_lists[r][:, half * 16 : (half + 1) * 16]
                 for b in range(2):
-                    nc.vector.tensor_tensor(terms[r][:, b, :], y_sb[b][:].indirect(offsets), gate_sb[:, r, tokens], MULT)
-            routed = held([P, 2, 256], F32, f"routed{half}")
-            nc.vector.tensor_tensor(routed[:], terms[0][:], terms[1][:], ADD)
-            total = held([P, 2, 256], F32, f"total{half}")
-            nc.vector.tensor_tensor(total[:], res[:], routed[:], ADD)
-            nc.sync.dma_start(out=out_rows[:, :, tokens], in_=total[:])
+                    k = 4 * half + 2 * r + b - 4
+                    pieces[r, b] = last[:, 0:256] if k == 3 else slots[k][:] if k >= 0 else held([P, 256], F32, f"term{half}_{r}_{b}")[:]
+                    nc.vector.tensor_tensor(pieces[r, b], y_sb[b][:].indirect(offsets), gate_sb[:, r, tokens], MULT)
+            partial = held([P, 512], F32, f"partial{half}")
+            for b in range(2):
+                cols = slice(b * 256, (b + 1) * 256)
+                nc.vector.tensor_tensor(partial[:, cols], bank[:, cols], pieces[0, b], ADD)
+            for b in range(2):
+                cols = slice(b * 256, (b + 1) * 256)
+                total = held([P, 256], F32, f"total{half}_{b}")
+                nc.vector.tensor_tensor(total[:], partial[:, cols], pieces[1, b], ADD)
+                nc.sync.dma_start(out=out_rows[:, b, tokens], in_=total[:])

@@ -21,14 +21,15 @@ ADD = mybir.AluOpType.add
 P = 128
 PASSES = K // 512
 SLOTS = E * C
+EARLY = 2
 GATHER_RUNS = [(0, 2), (2, 4), (4, 6), (6, 7), (7, 8)]
 GROUPS = [(0, 2), (2, 4), (4, 6), (6, 7), (7, 8)]
 SUM_BANKS = [0, 1, 2, 0, 1, 2, 0, 2]
 TURN_BANKS = [3, 4, 5, 6, 7]
-SHARED_BANKS = [2, 0, 1]
+SHARED_BANKS = [2, 0, 4]
 AHEAD = 1
 YS_BANKS = [2, 0]
-RESULT_BANKS = [1, 4, 5, 6, 7]
+RESULT_BANKS = [0, 4, 5, 6, 7]
 
 
 def tile_moe_shf_mlp_relu_kernel(
@@ -47,29 +48,30 @@ def tile_moe_shf_mlp_relu_kernel(
             engine.memset(plane[:].bitcast(I32), 0)
             return plane
 
-        def load_rows(plane, rows, which):
+        def load_rows(plane, rows, which, queue=nc.sync):
             for r in which:
-                nc.sync.dma_start(out=plane[:].bitcast(I32)[r:P:32], in_=rows[r].bitcast(I32))
+                queue.dma_start(out=plane[:].bitcast(I32)[r:P:32], in_=rows[r].bitcast(I32))
 
-        def load_packed(plane, scales, first):
+        def load_packed(plane, scales, first, queue):
             for q in range(4):
-                nc.sync.dma_start(
+                queue.dma_start(
                     out=plane[:].bitcast(I32)[32 * q + first : 32 * q + first + 8], in_=scales[:, 4 * q : 4 * q + 4, :].bitcast(I32)
                 )
 
         x_plane = zeroed_plane([P, PASSES, T], "x_plane", nc.gpsimd)
-        w1_plane = [zeroed_plane([P, 4 * PASSES, H], f"w1_plane{h}", nc.vector) for h in range(2)]
+        w1_plane = [zeroed_plane([P, count * PASSES, H], f"w1_plane{count}", nc.vector) for count in (E - EARLY, EARLY)][::-1]
         w2_plane = zeroed_plane([P, E, N], "w2_plane", nc.vector)
         w1s_plane = zeroed_plane([P, HS], "w1s_plane", nc.vector)
         w2s_plane = zeroed_plane([P, N], "w2s_plane", nc.vector)
         ident = held([P, P], F32, "ident")
         make_identity(nc, ident[:])
 
-        x_sb = held([P, PASSES, T], I32, "x_sb")
-        nc.sync.dma_start(out=x_sb[:], in_=x_words.rearrange("s p t d -> p s (t d)").bitcast(I32))
+        x_sb = [held([P, T], I32, f"x_sb{s}") for s in range(PASSES)]
+        nc.sync.dma_start(out=x_sb[0][:], in_=x_words[0].rearrange("p t d -> p (t d)").bitcast(I32))
         load_rows(x_plane, x_scales.rearrange("s (q r) t -> r q s t", r=4), range(4))
         slot_list = keep.tile([P, SLOTS // 16], U16, name="slot_list")
         nc.sync.dma_start(slot_list[:], offs)
+        nc.sync.dma_start(out=x_sb[1][:], in_=x_words[1].rearrange("p t d -> p (t d)").bitcast(I32))
         w1_sb = [held([P, 2 * PASSES, 2 * H], U8, f"w1_sb{i}") for i in range(E // 2)]
 
         def load_w1(i):
@@ -81,22 +83,22 @@ def tile_moe_shf_mlp_relu_kernel(
         token_lists = [keep.tile([P, T // 16], U16, name=f"token_list{r}") for r in range(2)]
         gate_sb = held([P, 2, T], F32, "gate_sb")
         w2s_sb = held([P, 2, N], I32, "w2s_sb")
+        load_rows(w1_plane[1], w1_scales[EARLY:E].rearrange("e s (q r) i -> r q (e s) i", r=4), range(4), nc.gpsimd)
+        load_rows(w2_plane, w2_scales.rearrange("e s (q r) n -> r q (e s) n", r=4), range(0, 4), nc.gpsimd)
+        load_packed(w1s_plane, w1s_scales, 4, nc.gpsimd)
         load_w1(0)
-        load_rows(w1_plane[0], w1_scales[0 : 4].rearrange("e s (q r) i -> r q (e s) i", r=4), range(4))
+        load_rows(w1_plane[0], w1_scales[0:EARLY].rearrange("e s (q r) i -> r q (e s) i", r=4), range(4), nc.sync)
         load_w1(1)
-        load_rows(w1_plane[1], w1_scales[4 : 8].rearrange("e s (q r) i -> r q (e s) i", r=4), range(4))
         load_w1(2)
-        load_rows(w2_plane, w2_scales.rearrange("e s (q r) n -> r q (e s) n", r=4), range(0, 4))
-        load_packed(w1s_plane, w1s_scales, 4)
-        nc.sync.dma_start(token_lists[0][:], pos1)
-        nc.sync.dma_start(token_lists[1][:], pos2)
         load_w1(3)
         nc.sync.dma_start(out=w2_sb[:].bitcast(I32), in_=w2_words.rearrange("e s p b -> p (e s) b").bitcast(I32))
+        nc.sync.dma_start(token_lists[0][:], pos1)
         nc.sync.dma_start(out=w1s_sb[0][:], in_=w1s_rows[:, :, 0:512])
         nc.sync.dma_start(out=gate_sb[:], in_=gate.rearrange("r p t -> p r t"))
+        nc.sync.dma_start(token_lists[1][:], pos2)
         nc.sync.dma_start(out=w1s_sb[1][:], in_=w1s_rows[:, :, 512:1024])
         nc.sync.dma_start(out=w2s_sb[:], in_=w2s_words.rearrange("s p n d -> p s (n d)").bitcast(I32))
-        load_packed(w2s_plane, w2s_scales, 8)
+        load_packed(w2s_plane, w2s_scales, 8, nc.sync)
 
         picked = {}
         for lo, hi in GATHER_RUNS:
@@ -105,7 +107,7 @@ def tile_moe_shf_mlp_relu_kernel(
             words = [held([P, n], U32, f"words{lo}_{s}") for s in range(PASSES)]
             scales = [held([P, n], U8, f"scales{lo}_{s}") for s in range(PASSES)]
             for s in range(PASSES):
-                nc.vector.tensor_copy(words[s][:], x_sb[:, s, :].bitcast(U32).indirect(offsets))
+                nc.vector.tensor_copy(words[s][:], x_sb[s][:].bitcast(U32).indirect(offsets))
                 nc.vector.tensor_copy(scales[s][:], x_plane[:, s, :].indirect(offsets))
             for e in range(lo, hi):
                 cols = slice((e - lo) * C, (e - lo + 1) * C)
@@ -137,7 +139,7 @@ def tile_moe_shf_mlp_relu_kernel(
             return codes, plane
 
         def routed_hidden(e):
-            weights = [(w1_sb[e // 2][:, (e % 2) * PASSES + s, :].bitcast(FP4X4), w1_plane[e // 4][:, (e % 4) * PASSES + s, :]) for s in range(PASSES)]
+            weights = [(w1_sb[e // 2][:, (e % 2) * PASSES + s, :].bitcast(FP4X4), w1_plane[0][:, e * PASSES + s, :] if e < EARLY else w1_plane[1][:, (e - EARLY) * PASSES + s, :]) for s in range(PASSES)]
             return first_layer(banks[SUM_BANKS[e]], picked[e], weights, held([P, 256], F32, f"hidden{e}")[:])
 
         y_sb = [held([P, SLOTS], F32, f"y_sb{b}") for b in range(2)]
@@ -176,10 +178,10 @@ def tile_moe_shf_mlp_relu_kernel(
         routed_sums(3)
         routed_codes(2)
         routed_sums(4)
-        routed_codes(3)
-        routed_codes(4)
         routed_results(0, *made[0])
+        routed_codes(3)
         routed_results(1, *made[1])
+        routed_codes(4)
         routed_results(2, *made[2])
         routed_results(3, *made[3])
         routed_results(4, *made[4])
@@ -191,13 +193,13 @@ def tile_moe_shf_mlp_relu_kernel(
             g, half, j = unit // 4, unit // 2 % 2, unit % 2
             weights = [(w1s_sb[g][:, s, :].bitcast(FP8X4), w1s_plane[4 + 4 * s :, g * 512 : (g + 1) * 512]) for s in range(PASSES)]
             cols = slice((2 * half + j) * P, (2 * half + j + 1) * P)
-            return first_layer(banks[SHARED_BANKS[unit % len(SHARED_BANKS)]], [(x_sb[:, s, cols], x_plane[:, s, cols]) for s in range(PASSES)], weights, slots[unit // 2 - 1][:] if j == 1 and unit > 1 else held([P, 256], F32, f"shared{unit}")[:])
+            return first_layer(banks[SHARED_BANKS[unit % len(SHARED_BANKS)]], [(x_sb[s][:, cols], x_plane[:, s, cols]) for s in range(PASSES)], weights, slots[unit // 2 - 1][:] if j == 1 and unit > 1 else held([P, 256], F32, f"shared{unit}")[:])
 
         shared = []
         units = []
         for pair in range(4):
             units.extend(shared_hidden(unit) for unit in range(len(units), min(2 * pair + 2 + AHEAD, 8)))
-            shared.append(turn_and_quantise(banks[3 + pair % 2], units[2 * pair : 2 * pair + 2], last[:] if pair == 3 else held([P, 512], F32, f"grouped_s{pair}")[:], f"hs{pair}"))
+            shared.append(turn_and_quantise(banks[1 + 2 * (pair % 2)], units[2 * pair : 2 * pair + 2], last[:] if pair == 3 else held([P, 512], F32, f"grouped_s{pair}")[:], f"hs{pair}"))
 
         out_rows = out.rearrange("(b p) t -> p b t", p=P)
         for half in range(2):

@@ -19,17 +19,18 @@ MULT = mybir.AluOpType.mult
 ADD = mybir.AluOpType.add
 
 P = 128
-PASSES = K // 512
+WIDTH = 512
+WORDS = WIDTH // 2
+PASSES = K // WIDTH
+SHARED_PASSES = HS // WIDTH
+BLOCKS = N // P
 SLOTS = E * C
-EARLY = 2
-GATHER_RUNS = [(0, 2), (2, 4), (4, 6), (6, 7), (7, 8)]
+HALF = T // 2
+PER_COLUMN = 16
 GROUPS = [(0, 2), (2, 4), (4, 6), (6, 7), (7, 8)]
-SUM_BANKS = [0, 1, 2, 0, 1, 2, 0, 2]
-TURN_BANKS = [3, 4, 5, 6, 7]
-SHARED_BANKS = [2, 0, 4]
-AHEAD = 1
-YS_BANKS = [2, 0]
-RESULT_BANKS = [0, 4, 5, 6, 7]
+SWAPPED = (1, 2)
+SUM_BANKS = 3
+W1S_FIRST, W2S_FIRST = 4, 8
 
 
 def tile_moe_shf_mlp_relu_kernel(
@@ -48,18 +49,19 @@ def tile_moe_shf_mlp_relu_kernel(
             engine.memset(plane[:].bitcast(I32), 0)
             return plane
 
-        def load_rows(plane, rows, which, queue=nc.sync):
-            for r in which:
+        def load_rows(queue, plane, rows):
+            for r in range(4):
                 queue.dma_start(out=plane[:].bitcast(I32)[r:P:32], in_=rows[r].bitcast(I32))
 
-        def load_packed(plane, scales, first, queue):
+        def load_stacked(queue, plane, scales, first):
             for q in range(4):
                 queue.dma_start(
                     out=plane[:].bitcast(I32)[32 * q + first : 32 * q + first + 8], in_=scales[:, 4 * q : 4 * q + 4, :].bitcast(I32)
                 )
 
         x_plane = zeroed_plane([P, PASSES, T], "x_plane", nc.gpsimd)
-        w1_plane = [zeroed_plane([P, count * PASSES, H], f"w1_plane{count}", nc.vector) for count in (E - EARLY, EARLY)][::-1]
+        w1_late_plane = zeroed_plane([P, E // 2 * PASSES, H], "w1_late_plane", nc.vector)
+        w1_early_plane = zeroed_plane([P, E // 2 * PASSES, H], "w1_early_plane", nc.vector)
         w2_plane = zeroed_plane([P, E, N], "w2_plane", nc.vector)
         w1s_plane = zeroed_plane([P, HS], "w1s_plane", nc.vector)
         w2s_plane = zeroed_plane([P, N], "w2s_plane", nc.vector)
@@ -68,44 +70,44 @@ def tile_moe_shf_mlp_relu_kernel(
 
         x_sb = [held([P, T], I32, f"x_sb{s}") for s in range(PASSES)]
         nc.sync.dma_start(out=x_sb[0][:], in_=x_words[0].rearrange("p t d -> p (t d)").bitcast(I32))
-        load_rows(x_plane, x_scales.rearrange("s (q r) t -> r q s t", r=4), range(4))
-        slot_list = keep.tile([P, SLOTS // 16], U16, name="slot_list")
+        load_rows(nc.sync, x_plane, x_scales.rearrange("s (q r) t -> r q s t", r=4))
+        slot_list = keep.tile([P, SLOTS // PER_COLUMN], U16, name="slot_list")
         nc.sync.dma_start(slot_list[:], offs)
         nc.sync.dma_start(out=x_sb[1][:], in_=x_words[1].rearrange("p t d -> p (t d)").bitcast(I32))
-        w1_sb = [held([P, 2 * PASSES, 2 * H], U8, f"w1_sb{i}") for i in range(E // 2)]
 
-        def load_w1(i):
-            nc.sync.dma_start(out=w1_sb[i][:].bitcast(I32), in_=w1_words[2 * i : 2 * i + 2].rearrange("e s p b -> p (e s) b").bitcast(I32))
+        load_rows(nc.gpsimd, w1_late_plane, w1_scales[E // 2 :].rearrange("e s (q r) i -> r q (e s) i", r=4))
+        load_stacked(nc.gpsimd, w1s_plane, w1s_scales, W1S_FIRST)
 
-        w2_sb = held([P, E, 2 * N], U8, "w2_sb")
-        w1s_sb = [held([P, PASSES, 512], I32, f"w1s_sb{g}") for g in range(2)]
+        load_rows(nc.sync, w1_early_plane, w1_scales[: E // 2].rearrange("e s (q r) i -> r q (e s) i", r=4))
+        w1_sb = [held([P, PASSES, 2 * H], U8, f"w1_sb{e}") for e in range(E)]
+        for e in range(E):
+            nc.sync.dma_start(out=w1_sb[e][:].bitcast(I32), in_=w1_words[e].rearrange("s p b -> p s b").bitcast(I32))
+        load_rows(nc.sync, w2_plane, w2_scales.rearrange("e s (q r) n -> r q (e s) n", r=4))
+        w2_sb = [held([P, E // 2, 2 * N], U8, f"w2_sb{part}") for part in range(2)]
+        for part in range(2):
+            experts = w2_words[part * E // 2 : (part + 1) * E // 2]
+            nc.sync.dma_start(out=w2_sb[part][:].bitcast(I32), in_=experts.rearrange("e s p b -> p (e s) b").bitcast(I32))
+
+        w1s_sb = [held([P, PASSES, WIDTH], I32, f"w1s_sb{g}") for g in range(SHARED_PASSES)]
         w1s_rows = w1s_words.rearrange("s p l d -> p s (l d)").bitcast(I32)
-        token_lists = [keep.tile([P, T // 16], U16, name=f"token_list{r}") for r in range(2)]
-        gate_sb = held([P, 2, T], F32, "gate_sb")
-        w2s_sb = held([P, 2, N], I32, "w2s_sb")
-        load_rows(w1_plane[1], w1_scales[EARLY:E].rearrange("e s (q r) i -> r q (e s) i", r=4), range(4), nc.gpsimd)
-        load_rows(w2_plane, w2_scales.rearrange("e s (q r) n -> r q (e s) n", r=4), range(0, 4), nc.gpsimd)
-        load_packed(w1s_plane, w1s_scales, 4, nc.gpsimd)
-        load_w1(0)
-        load_rows(w1_plane[0], w1_scales[0:EARLY].rearrange("e s (q r) i -> r q (e s) i", r=4), range(4), nc.sync)
-        load_w1(1)
-        load_w1(2)
-        load_w1(3)
-        nc.sync.dma_start(out=w2_sb[:].bitcast(I32), in_=w2_words.rearrange("e s p b -> p (e s) b").bitcast(I32))
-        nc.sync.dma_start(token_lists[0][:], pos1)
-        nc.sync.dma_start(out=w1s_sb[0][:], in_=w1s_rows[:, :, 0:512])
-        nc.sync.dma_start(out=gate_sb[:], in_=gate.rearrange("r p t -> p r t"))
-        nc.sync.dma_start(token_lists[1][:], pos2)
-        nc.sync.dma_start(out=w1s_sb[1][:], in_=w1s_rows[:, :, 512:1024])
+        token_lists = [keep.tile([P, T // PER_COLUMN], U16, name=f"token_list{r}") for r in range(2)]
+        gate_sb = [[held([P, HALF], F32, f"gate_sb{half}_{r}") for r in range(2)] for half in range(2)]
+        nc.sync.dma_start(out=w1s_sb[0][:], in_=w1s_rows[:, :, :WIDTH])
+        for r, pos in enumerate((pos1, pos2)):
+            nc.sync.dma_start(token_lists[r][:], pos)
+            nc.sync.dma_start(out=gate_sb[0][r][:], in_=gate[r, :, :HALF])
+        nc.sync.dma_start(out=w1s_sb[1][:], in_=w1s_rows[:, :, WIDTH:])
+        for r in range(2):
+            nc.sync.dma_start(out=gate_sb[1][r][:], in_=gate[r, :, HALF:])
+        w2s_sb = held([P, SHARED_PASSES, N], I32, "w2s_sb")
         nc.sync.dma_start(out=w2s_sb[:], in_=w2s_words.rearrange("s p n d -> p s (n d)").bitcast(I32))
-        load_packed(w2s_plane, w2s_scales, 8, nc.sync)
+        load_stacked(nc.sync, w2s_plane, w2s_scales, W2S_FIRST)
 
         picked = {}
-        for lo, hi in GATHER_RUNS:
-            n = (hi - lo) * C
-            offsets = slot_list[:, lo * C // 16 : hi * C // 16]
-            words = [held([P, n], U32, f"words{lo}_{s}") for s in range(PASSES)]
-            scales = [held([P, n], U8, f"scales{lo}_{s}") for s in range(PASSES)]
+        for lo, hi in GROUPS:
+            offsets = slot_list[:, lo * C // PER_COLUMN : hi * C // PER_COLUMN]
+            words = [held([P, (hi - lo) * C], U32, f"words{lo}_{s}") for s in range(PASSES)]
+            scales = [held([P, (hi - lo) * C], U8, f"scales{lo}_{s}") for s in range(PASSES)]
             for s in range(PASSES):
                 nc.vector.tensor_copy(words[s][:], x_sb[s][:].bitcast(U32).indirect(offsets))
                 nc.vector.tensor_copy(scales[s][:], x_plane[:, s, :].indirect(offsets))
@@ -113,119 +115,103 @@ def tile_moe_shf_mlp_relu_kernel(
                 cols = slice((e - lo) * C, (e - lo + 1) * C)
                 picked[e] = [(words[s][:, cols], scales[s][:, cols]) for s in range(PASSES)]
 
-        banks = [psum.tile([P, 512], F32, name=f"bank{b}") for b in range(8)]
+        banks = [psum.tile([P, WIDTH], F32, name=f"bank{b}") for b in range(8)]
 
-        def first_layer(acc, tokens, weights, hidden):
+        def first_layer(unit, tokens, weights):
+            acc = banks[unit % SUM_BANKS]
             for s in range(PASSES):
                 nc.tensor.matmul_mx(
                     out=acc[:], lhsT=tokens[s][0].bitcast(FP8X4), lhsT_scale=tokens[s][1],
                     rhs=weights[s][0], rhs_scale=weights[s][1], start=(s == 0), stop=(s == PASSES - 1),
                 )
+            hidden = held([P, WORDS], F32, f"hidden{unit}")
             nc.scalar.activation(
-                out=hidden.bitcast(BF16).rearrange("s (u p e) -> s u p e", u=2, e=2), in_=acc[:].rearrange("s (p u e) -> s u p e", u=2, e=2), func=RELU
+                out=hidden[:].bitcast(BF16).rearrange("s (u p e) -> s u p e", u=2, e=2),
+                in_=acc[:].rearrange("s (p u e) -> s u p e", u=2, e=2),
+                func=RELU,
             )
             return hidden
 
-        def turn_and_quantise(bank, hiddens, grouped, name):
+        def turn_and_quantise(bank, hiddens, copy, name):
             count = len(hiddens)
-            turned = bank[:, 0 : count * 256].rearrange("p (j u s) -> p j u s", j=count, u=2)
+            turned = bank[:, : count * WORDS].rearrange("p (j u s) -> p j u s", j=count, u=2)
             for j in reversed(range(count)):
                 for u in range(2):
                     nc.tensor.transpose(turned[:, j, u, :], hiddens[j][:, u * P : (u + 1) * P], ident[:])
-            nc.scalar.copy(out=grouped.rearrange("p (j s u) -> p j s u", j=count, u=2), in_=turned.rearrange("p j u s -> p j s u"))
+            grouped = held([P, count * WORDS], F32, f"grouped_{name}")
+            copy(out=grouped[:].rearrange("p (j s u) -> p j s u", j=count, u=2), in_=turned.rearrange("p j u s -> p j s u"))
             codes = held([P, count * P], U32, f"codes_{name}")
             plane = held([P, count * P], U8, f"plane_{name}")
-            nc.vector.quantize_mx(out=codes[:].bitcast(FP8X4), scales=plane[:], in_=grouped.bitcast(BF16))
+            nc.vector.quantize_mx(out=codes[:].bitcast(FP8X4), scales=plane[:], in_=grouped[:].bitcast(BF16))
             return codes, plane
 
-        def routed_hidden(e):
-            weights = [(w1_sb[e // 2][:, (e % 2) * PASSES + s, :].bitcast(FP4X4), w1_plane[0][:, e * PASSES + s, :] if e < EARLY else w1_plane[1][:, (e - EARLY) * PASSES + s, :]) for s in range(PASSES)]
-            return first_layer(banks[SUM_BANKS[e]], picked[e], weights, held([P, 256], F32, f"hidden{e}")[:])
+        def routed_sums(e):
+            plane = w1_early_plane if e < E // 2 else w1_late_plane
+            weights = [(w1_sb[e][:, s, :].bitcast(FP4X4), plane[:, e % (E // 2) * PASSES + s, :]) for s in range(PASSES)]
+            return first_layer(e, picked[e], weights)
 
-        y_sb = [held([P, SLOTS], F32, f"y_sb{b}") for b in range(2)]
+        hiddens, routed_codes = [], []
+        for i, (lo, hi) in enumerate(GROUPS):
+            hiddens.extend(routed_sums(e) for e in range(len(hiddens), min(hi + 2, E)))
+            copy = nc.vector.tensor_copy if i in SWAPPED else nc.scalar.copy
+            routed_codes.append(turn_and_quantise(banks[SUM_BANKS + i], hiddens[lo:hi], copy, f"h{i}"))
 
-        def routed_results(group, codes, plane):
-            lo, hi = GROUPS[group]
-            bank = banks[RESULT_BANKS[group]]
-            for b in range(2):
+        y_sb = [held([P, SLOTS], F32, f"y_sb{b}") for b in range(BLOCKS)]
+        for i, (lo, hi) in enumerate(GROUPS):
+            codes, plane = routed_codes[i]
+            results = banks[SUM_BANKS + i][:].rearrange("p (b j) -> p b j", b=BLOCKS)
+            for b in range(BLOCKS):
                 for e in range(lo, hi):
-                    j = e - lo
+                    cols = slice((e - lo) * C, (e - lo + 1) * C)
                     nc.tensor.matmul_mx(
-                        out=bank[:, b * 256 + j * C : b * 256 + (j + 1) * C],
-                        lhsT=w2_sb[:, e, b * 256 : (b + 1) * 256].bitcast(FP4X4), lhsT_scale=w2_plane[:, e, b * P : (b + 1) * P],
-                        rhs=codes[:, j * C : (j + 1) * C].bitcast(FP8X4), rhs_scale=plane[:, j * C : (j + 1) * C], start=True, stop=True,
+                        out=results[:, b, cols],
+                        lhsT=w2_sb[e // (E // 2)][:, e % (E // 2), 2 * b * P : 2 * (b + 1) * P].bitcast(FP4X4),
+                        lhsT_scale=w2_plane[:, e, b * P : (b + 1) * P],
+                        rhs=codes[:, cols].bitcast(FP8X4), rhs_scale=plane[:, cols], start=True, stop=True,
                     )
-            for b in range(2):
-                copy = nc.scalar.copy if (group, b) in [] else nc.vector.tensor_copy
-                copy(y_sb[b][:, lo * C : hi * C], bank[:, b * 256 : b * 256 + (hi - lo) * C])
+            copy = nc.scalar.copy if i in SWAPPED else nc.vector.tensor_copy
+            for b in range(BLOCKS):
+                copy(y_sb[b][:, lo * C : hi * C], results[:, b, : (hi - lo) * C])
 
-        hiddens, made = {}, {}
+        def shared_sums(index):
+            g, tile = index // 4, index % 4
+            first = [W1S_FIRST + 4 * s for s in range(PASSES)]
+            weights = [(w1s_sb[g][:, s, :].bitcast(FP8X4), w1s_plane[first[s] :, g * WIDTH : (g + 1) * WIDTH]) for s in range(PASSES)]
+            cols = slice(tile * P, (tile + 1) * P)
+            return first_layer(E + index, [(x_sb[s][:, cols], x_plane[:, s, cols]) for s in range(PASSES)], weights)
 
-        def routed_sums(group):
-            for e in range(*GROUPS[group]):
-                hiddens[e] = routed_hidden(e)
+        pairs = 2 * SHARED_PASSES
+        shared_hiddens, shared_codes = [], []
+        for pair in range(pairs):
+            shared_hiddens.extend(shared_sums(index) for index in range(len(shared_hiddens), min(2 * pair + 3, 2 * pairs)))
+            units = shared_hiddens[2 * pair : 2 * pair + 2]
+            shared_codes.append(turn_and_quantise(banks[SUM_BANKS + pair % 2], units, nc.scalar.copy, f"hs{pair}"))
 
-        def routed_codes(group):
-            lo, hi = GROUPS[group]
-            grouped = held([P, (hi - lo) * 256], F32, f"grouped{group}")
-            made[group] = turn_and_quantise(banks[TURN_BANKS[group]], [hiddens[e] for e in range(lo, hi)], grouped[:], f"h{group}")
-
-        routed_sums(0)
-        routed_sums(1)
-        routed_codes(0)
-        routed_sums(2)
-        routed_codes(1)
-        routed_sums(3)
-        routed_codes(2)
-        routed_sums(4)
-        routed_results(0, *made[0])
-        routed_codes(3)
-        routed_results(1, *made[1])
-        routed_codes(4)
-        routed_results(2, *made[2])
-        routed_results(3, *made[3])
-        routed_results(4, *made[4])
-
-        slots = [held([P, 256], F32, f"slot{k}") for k in range(3)]
-        last = held([P, 512], F32, "last")
-
-        def shared_hidden(unit):
-            g, half, j = unit // 4, unit // 2 % 2, unit % 2
-            weights = [(w1s_sb[g][:, s, :].bitcast(FP8X4), w1s_plane[4 + 4 * s :, g * 512 : (g + 1) * 512]) for s in range(PASSES)]
-            cols = slice((2 * half + j) * P, (2 * half + j + 1) * P)
-            return first_layer(banks[SHARED_BANKS[unit % len(SHARED_BANKS)]], [(x_sb[s][:, cols], x_plane[:, s, cols]) for s in range(PASSES)], weights, slots[unit // 2 - 1][:] if j == 1 and unit > 1 else held([P, 256], F32, f"shared{unit}")[:])
-
-        shared = []
-        units = []
-        for pair in range(4):
-            units.extend(shared_hidden(unit) for unit in range(len(units), min(2 * pair + 2 + AHEAD, 8)))
-            shared.append(turn_and_quantise(banks[1 + 2 * (pair % 2)], units[2 * pair : 2 * pair + 2], last[:] if pair == 3 else held([P, 512], F32, f"grouped_s{pair}")[:], f"hs{pair}"))
-
+        shared_banks = [banks[5], banks[6], banks[7], banks[2]]
         out_rows = out.rearrange("(b p) t -> p b t", p=P)
         for half in range(2):
-            bank = banks[YS_BANKS[half]]
-            for b in range(2):
-                for g in range(2):
-                    codes, plane = shared[2 * g + half]
+            shared = [shared_banks[BLOCKS * half + b][:, :HALF] for b in range(BLOCKS)]
+            for b in range(BLOCKS):
+                for g in range(SHARED_PASSES):
+                    codes, plane = shared_codes[2 * g + half]
                     nc.tensor.matmul_mx(
-                        out=bank[:, b * 256 : (b + 1) * 256],
-                        lhsT=w2s_sb[:, g, b * P : (b + 1) * P].bitcast(FP8X4), lhsT_scale=w2s_plane[8 + 4 * g :, b * P : (b + 1) * P],
-                        rhs=codes[:].bitcast(FP8X4), rhs_scale=plane[:], start=(g == 0), stop=(g == 1),
+                        out=shared[b],
+                        lhsT=w2s_sb[:, g, b * P : (b + 1) * P].bitcast(FP8X4),
+                        lhsT_scale=w2s_plane[W2S_FIRST + 4 * g :, b * P : (b + 1) * P],
+                        rhs=codes[:].bitcast(FP8X4), rhs_scale=plane[:], start=(g == 0), stop=(g == SHARED_PASSES - 1),
                     )
-            tokens = slice(half * 256, (half + 1) * 256)
-            pieces = {}
+            terms = []
             for r in range(2):
-                offsets = token_lists[r][:, half * 16 : (half + 1) * 16]
-                for b in range(2):
-                    k = 4 * half + 2 * r + b - 4
-                    pieces[r, b] = last[:, 0:256] if k == 3 else slots[k][:] if k >= 0 else held([P, 256], F32, f"term{half}_{r}_{b}")[:]
-                    nc.vector.tensor_tensor(pieces[r, b], y_sb[b][:].indirect(offsets), gate_sb[:, r, tokens], MULT)
-            partial = held([P, 512], F32, f"partial{half}")
-            for b in range(2):
-                cols = slice(b * 256, (b + 1) * 256)
-                nc.vector.tensor_tensor(partial[:, cols], bank[:, cols], pieces[0, b], ADD)
-            for b in range(2):
-                cols = slice(b * 256, (b + 1) * 256)
-                total = held([P, 256], F32, f"total{half}_{b}")
-                nc.vector.tensor_tensor(total[:], partial[:, cols], pieces[1, b], ADD)
-                nc.sync.dma_start(out=out_rows[:, b, tokens], in_=total[:])
+                offsets = token_lists[r][:, half * HALF // PER_COLUMN : (half + 1) * HALF // PER_COLUMN]
+                if (half, r) == (1, 1):
+                    terms.append([shared_hiddens[2 * (pairs - BLOCKS + b) + 1] for b in range(BLOCKS)])
+                else:
+                    terms.append([held([P, HALF], F32, f"term{half}_{r}_{b}") for b in range(BLOCKS)])
+                for b in range(BLOCKS):
+                    nc.vector.tensor_tensor(terms[r][b][:], y_sb[b][:].indirect(offsets), gate_sb[half][r][:], MULT)
+            for b in range(BLOCKS):
+                routed = held([P, HALF], F32, f"routed{half}_{b}")
+                nc.vector.tensor_tensor(routed[:], terms[0][b][:], terms[1][b][:], ADD)
+                total = held([P, HALF], F32, f"total{half}_{b}")
+                nc.vector.tensor_tensor(total[:], shared[b], routed[:], ADD)
+                nc.sync.dma_start(out=out_rows[:, b, half * HALF : (half + 1) * HALF], in_=total[:])

@@ -30,7 +30,8 @@ PER_COLUMN = 16
 GROUPS = [(0, 2), (2, 4), (4, 6), (6, 7), (7, 8)]
 SWAPPED = (1, 2)
 SUM_BANKS = 3
-W1S_FIRST, W2S_FIRST = 4, 8
+SHARED_FIRST = 8
+LIFT_BEFORE = 2
 
 
 def tile_moe_shf_mlp_relu_kernel(
@@ -59,28 +60,47 @@ def tile_moe_shf_mlp_relu_kernel(
                     out=plane[:].bitcast(I32)[32 * q + first : 32 * q + first + 8], in_=scales[:, 4 * q : 4 * q + 4, :].bitcast(I32)
                 )
 
-        x_plane = zeroed_plane([P, PASSES, T], "x_plane", nc.gpsimd)
+        x_plane = zeroed_plane([P, T], "x_plane", nc.gpsimd)
         w1_late_plane = zeroed_plane([P, E // 2 * PASSES, H], "w1_late_plane", nc.vector)
         w1_early_plane = zeroed_plane([P, E // 2 * PASSES, H], "w1_early_plane", nc.vector)
         w2_plane = zeroed_plane([P, E, N], "w2_plane", nc.vector)
         w1s_plane = zeroed_plane([P, HS], "w1s_plane", nc.vector)
         w2s_plane = zeroed_plane([P, N], "w2s_plane", nc.vector)
+        lifted = zeroed_plane([P, SLOTS], "lifted", nc.vector)
         ident = held([P, P], F32, "ident")
         make_identity(nc, ident[:])
 
         x_sb = [held([P, T], I32, f"x_sb{s}") for s in range(PASSES)]
         nc.sync.dma_start(out=x_sb[0][:], in_=x_words[0].rearrange("p t d -> p (t d)").bitcast(I32))
-        load_rows(nc.sync, x_plane, x_scales.rearrange("s (q r) t -> r q s t", r=4))
+        load_stacked(nc.sync, x_plane, x_scales, 0)
         slot_list = keep.tile([P, SLOTS // PER_COLUMN], U16, name="slot_list")
         nc.sync.dma_start(slot_list[:], offs)
         nc.sync.dma_start(out=x_sb[1][:], in_=x_words[1].rearrange("p t d -> p (t d)").bitcast(I32))
 
         load_rows(nc.gpsimd, w1_late_plane, w1_scales[E // 2 :].rearrange("e s (q r) i -> r q (e s) i", r=4))
-        load_stacked(nc.gpsimd, w1s_plane, w1s_scales, W1S_FIRST)
+        load_stacked(nc.gpsimd, w1s_plane, w1s_scales, SHARED_FIRST)
 
         load_rows(nc.sync, w1_early_plane, w1_scales[: E // 2].rearrange("e s (q r) i -> r q (e s) i", r=4))
         w1_sb = [held([P, PASSES, 2 * H], U8, f"w1_sb{e}") for e in range(E)]
+        stacked = held([P, SLOTS], U8, "stacked")
+        words = {}
+
+        def gather_scales():
+            for lo in range(0, SLOTS, 2 * C):
+                offsets = slot_list[:, lo // PER_COLUMN : (lo + 2 * C) // PER_COLUMN]
+                nc.vector.tensor_copy(stacked[:, lo : lo + 2 * C], x_plane[:].indirect(offsets))
+            for r in range(4):
+                nc.sync.dma_start(out=lifted[:].bitcast(I32)[r:P:32], in_=stacked[:].bitcast(I32)[4 + r : P : 32])
+
+        def gather_words(lo, hi):
+            offsets = slot_list[:, lo * C // PER_COLUMN : hi * C // PER_COLUMN]
+            for s in range(PASSES):
+                words[lo, s] = held([P, (hi - lo) * C], U32, f"words{lo}_{s}")
+                nc.vector.tensor_copy(words[lo, s][:], x_sb[s][:].bitcast(U32).indirect(offsets))
+
         for e in range(E):
+            if e == LIFT_BEFORE:
+                gather_scales()
             nc.sync.dma_start(out=w1_sb[e][:].bitcast(I32), in_=w1_words[e].rearrange("s p b -> p s b").bitcast(I32))
         load_rows(nc.sync, w2_plane, w2_scales.rearrange("e s (q r) n -> r q (e s) n", r=4))
         w2_sb = [held([P, E // 2, 2 * N], U8, f"w2_sb{part}") for part in range(2)]
@@ -93,27 +113,22 @@ def tile_moe_shf_mlp_relu_kernel(
         token_lists = [keep.tile([P, T // PER_COLUMN], U16, name=f"token_list{r}") for r in range(2)]
         gate_sb = [[held([P, HALF], F32, f"gate_sb{half}_{r}") for r in range(2)] for half in range(2)]
         nc.sync.dma_start(out=w1s_sb[0][:], in_=w1s_rows[:, :, :WIDTH])
+        nc.sync.dma_start(out=w1s_sb[1][:], in_=w1s_rows[:, :, WIDTH:])
         for r, pos in enumerate((pos1, pos2)):
             nc.sync.dma_start(token_lists[r][:], pos)
             nc.sync.dma_start(out=gate_sb[0][r][:], in_=gate[r, :, :HALF])
-        nc.sync.dma_start(out=w1s_sb[1][:], in_=w1s_rows[:, :, WIDTH:])
         for r in range(2):
             nc.sync.dma_start(out=gate_sb[1][r][:], in_=gate[r, :, HALF:])
         w2s_sb = held([P, SHARED_PASSES, N], I32, "w2s_sb")
         nc.sync.dma_start(out=w2s_sb[:], in_=w2s_words.rearrange("s p n d -> p s (n d)").bitcast(I32))
-        load_stacked(nc.sync, w2s_plane, w2s_scales, W2S_FIRST)
+        load_stacked(nc.sync, w2s_plane, w2s_scales, SHARED_FIRST)
 
         picked = {}
         for lo, hi in GROUPS:
-            offsets = slot_list[:, lo * C // PER_COLUMN : hi * C // PER_COLUMN]
-            words = [held([P, (hi - lo) * C], U32, f"words{lo}_{s}") for s in range(PASSES)]
-            scales = [held([P, (hi - lo) * C], U8, f"scales{lo}_{s}") for s in range(PASSES)]
-            for s in range(PASSES):
-                nc.vector.tensor_copy(words[s][:], x_sb[s][:].bitcast(U32).indirect(offsets))
-                nc.vector.tensor_copy(scales[s][:], x_plane[:, s, :].indirect(offsets))
+            gather_words(lo, hi)
             for e in range(lo, hi):
                 cols = slice((e - lo) * C, (e - lo + 1) * C)
-                picked[e] = [(words[s][:, cols], scales[s][:, cols]) for s in range(PASSES)]
+                picked[e] = [(words[lo, s][:, cols], plane[:, e * C : (e + 1) * C]) for s, plane in enumerate((stacked, lifted))]
 
         banks = [psum.tile([P, WIDTH], F32, name=f"bank{b}") for b in range(8)]
 
@@ -125,11 +140,12 @@ def tile_moe_shf_mlp_relu_kernel(
                     rhs=weights[s][0], rhs_scale=weights[s][1], start=(s == 0), stop=(s == PASSES - 1),
                 )
             hidden = held([P, WORDS], F32, f"hidden{unit}")
-            nc.scalar.activation(
-                out=hidden[:].bitcast(BF16).rearrange("s (u p e) -> s u p e", u=2, e=2),
-                in_=acc[:].rearrange("s (p u e) -> s u p e", u=2, e=2),
-                func=RELU,
-            )
+            rounded = hidden[:].bitcast(BF16).rearrange("s (u p e) -> s u p e", u=2, e=2)
+            sums = acc[:].rearrange("s (p u e) -> s u p e", u=2, e=2)
+            if unit == E - 1:
+                nc.vector.tensor_scalar_max(rounded, sums, 0.0)
+            else:
+                nc.scalar.activation(out=rounded, in_=sums, func=RELU)
             return hidden
 
         def turn_and_quantise(bank, hiddens, copy, name):
@@ -175,10 +191,10 @@ def tile_moe_shf_mlp_relu_kernel(
 
         def shared_sums(index):
             g, tile = index // 4, index % 4
-            first = [W1S_FIRST + 4 * s for s in range(PASSES)]
+            first = [SHARED_FIRST + 4 * s for s in range(PASSES)]
             weights = [(w1s_sb[g][:, s, :].bitcast(FP8X4), w1s_plane[first[s] :, g * WIDTH : (g + 1) * WIDTH]) for s in range(PASSES)]
             cols = slice(tile * P, (tile + 1) * P)
-            return first_layer(E + index, [(x_sb[s][:, cols], x_plane[:, s, cols]) for s in range(PASSES)], weights)
+            return first_layer(E + index, [(x_sb[s][:, cols], x_plane[4 * s :, cols]) for s in range(PASSES)], weights)
 
         pairs = 2 * SHARED_PASSES
         shared_hiddens, shared_codes = [], []
@@ -197,7 +213,7 @@ def tile_moe_shf_mlp_relu_kernel(
                     nc.tensor.matmul_mx(
                         out=shared[b],
                         lhsT=w2s_sb[:, g, b * P : (b + 1) * P].bitcast(FP8X4),
-                        lhsT_scale=w2s_plane[W2S_FIRST + 4 * g :, b * P : (b + 1) * P],
+                        lhsT_scale=w2s_plane[SHARED_FIRST + 4 * g :, b * P : (b + 1) * P],
                         rhs=codes[:].bitcast(FP8X4), rhs_scale=plane[:], start=(g == 0), stop=(g == SHARED_PASSES - 1),
                     )
             terms = []

@@ -25,13 +25,16 @@ PASSES = K // WIDTH
 SHARED_PASSES = HS // WIDTH
 BLOCKS = N // P
 SLOTS = E * C
+TILES = T // P
 HALF = T // 2
 PER_COLUMN = 16
 GROUPS = [(0, 2), (2, 4), (4, 6), (6, 7), (7, 8)]
-SWAPPED = (1, 2)
-SUM_BANKS = 3
+SUM_BANKS = 4
+TURN_BANKS = (4, 2, 6, 7, 4)
+VECTOR_TURNS = (1, 3)
+RESULT_RUNS = [(0, 4, 0), (4, 7, 5)]
 SHARED_FIRST = 8
-LIFT_BEFORE = 2
+LIFT_BEFORE = 1
 
 
 def tile_moe_shf_mlp_relu_kernel(
@@ -50,184 +53,175 @@ def tile_moe_shf_mlp_relu_kernel(
             engine.memset(plane[:].bitcast(I32), 0)
             return plane
 
-        def load_rows(queue, plane, rows):
-            for r in range(4):
+        def load_rows(queues, plane, rows):
+            for r, queue in enumerate(queues):
                 queue.dma_start(out=plane[:].bitcast(I32)[r:P:32], in_=rows[r].bitcast(I32))
 
-        def load_stacked(queue, plane, scales, first):
+        def load_stacked(plane, scales, first):
             for q in range(4):
-                queue.dma_start(
+                nc.sync.dma_start(
                     out=plane[:].bitcast(I32)[32 * q + first : 32 * q + first + 8], in_=scales[:, 4 * q : 4 * q + 4, :].bitcast(I32)
                 )
 
         x_plane = zeroed_plane([P, T], "x_plane", nc.gpsimd)
-        w1_late_plane = zeroed_plane([P, E // 2 * PASSES, H], "w1_late_plane", nc.vector)
-        w1_early_plane = zeroed_plane([P, E // 2 * PASSES, H], "w1_early_plane", nc.vector)
-        w2_plane = zeroed_plane([P, E, N], "w2_plane", nc.vector)
+        w1_plane = zeroed_plane([P, E * PASSES, H], "w1_plane", nc.vector)
         w1s_plane = zeroed_plane([P, HS], "w1s_plane", nc.vector)
-        w2s_plane = zeroed_plane([P, N], "w2s_plane", nc.vector)
         lifted = zeroed_plane([P, SLOTS], "lifted", nc.vector)
+        w2_plane = zeroed_plane([P, E, N], "w2_plane", nc.vector)
+        w2s_plane = zeroed_plane([P, N], "w2s_plane", nc.vector)
         ident = held([P, P], F32, "ident")
         make_identity(nc, ident[:])
 
-        x_sb = [held([P, T], I32, f"x_sb{s}") for s in range(PASSES)]
-        nc.sync.dma_start(out=x_sb[0][:], in_=x_words[0].rearrange("p t d -> p (t d)").bitcast(I32))
-        load_stacked(nc.sync, x_plane, x_scales, 0)
         slot_list = keep.tile([P, SLOTS // PER_COLUMN], U16, name="slot_list")
+        x_sb = held([P, PASSES, T], I32, "x_sb")
+        nc.sync.dma_start(out=x_sb[:], in_=x_words.rearrange("s p t d -> p s (t d)").bitcast(I32))
+        load_stacked(x_plane, x_scales, 0)
         nc.sync.dma_start(slot_list[:], offs)
-        nc.sync.dma_start(out=x_sb[1][:], in_=x_words[1].rearrange("p t d -> p (t d)").bitcast(I32))
-
-        load_rows(nc.gpsimd, w1_late_plane, w1_scales[E // 2 :].rearrange("e s (q r) i -> r q (e s) i", r=4))
-        load_stacked(nc.gpsimd, w1s_plane, w1s_scales, SHARED_FIRST)
-
-        load_rows(nc.sync, w1_early_plane, w1_scales[: E // 2].rearrange("e s (q r) i -> r q (e s) i", r=4))
-        w1_sb = [held([P, PASSES, 2 * H], U8, f"w1_sb{e}") for e in range(E)]
-        stacked = held([P, SLOTS], U8, "stacked")
-        words = {}
-
-        def gather_scales():
-            for lo in range(0, SLOTS, 2 * C):
-                offsets = slot_list[:, lo // PER_COLUMN : (lo + 2 * C) // PER_COLUMN]
-                nc.vector.tensor_copy(stacked[:, lo : lo + 2 * C], x_plane[:].indirect(offsets))
-            for r in range(4):
-                nc.sync.dma_start(out=lifted[:].bitcast(I32)[r:P:32], in_=stacked[:].bitcast(I32)[4 + r : P : 32])
-
-        def gather_words(lo, hi):
-            offsets = slot_list[:, lo * C // PER_COLUMN : hi * C // PER_COLUMN]
-            for s in range(PASSES):
-                words[lo, s] = held([P, (hi - lo) * C], U32, f"words{lo}_{s}")
-                nc.vector.tensor_copy(words[lo, s][:], x_sb[s][:].bitcast(U32).indirect(offsets))
-
-        for e in range(E):
-            if e == LIFT_BEFORE:
-                gather_scales()
-            nc.sync.dma_start(out=w1_sb[e][:].bitcast(I32), in_=w1_words[e].rearrange("s p b -> p s b").bitcast(I32))
-        load_rows(nc.sync, w2_plane, w2_scales.rearrange("e s (q r) n -> r q (e s) n", r=4))
-        w2_sb = [held([P, E // 2, 2 * N], U8, f"w2_sb{part}") for part in range(2)]
-        for part in range(2):
-            experts = w2_words[part * E // 2 : (part + 1) * E // 2]
-            nc.sync.dma_start(out=w2_sb[part][:].bitcast(I32), in_=experts.rearrange("e s p b -> p (e s) b").bitcast(I32))
-
         w1s_sb = [held([P, PASSES, WIDTH], I32, f"w1s_sb{g}") for g in range(SHARED_PASSES)]
         w1s_rows = w1s_words.rearrange("s p l d -> p s (l d)").bitcast(I32)
-        token_lists = [keep.tile([P, T // PER_COLUMN], U16, name=f"token_list{r}") for r in range(2)]
-        gate_sb = [[held([P, HALF], F32, f"gate_sb{half}_{r}") for r in range(2)] for half in range(2)]
         nc.sync.dma_start(out=w1s_sb[0][:], in_=w1s_rows[:, :, :WIDTH])
-        nc.sync.dma_start(out=w1s_sb[1][:], in_=w1s_rows[:, :, WIDTH:])
+        load_stacked(w1s_plane, w1s_scales, SHARED_FIRST)
+        load_rows([nc.gpsimd, nc.gpsimd, nc.sync, nc.sync], w1_plane, w1_scales.rearrange("e s (q r) i -> r q (e s) i", r=4))
+
+        stacked = held([P, SLOTS], U8, "stacked")
+        for lo in range(0, SLOTS, 2 * C):
+            offsets = slot_list[:, lo // PER_COLUMN : (lo + 2 * C) // PER_COLUMN]
+            nc.vector.tensor_copy(stacked[:, lo : lo + 2 * C], x_plane[:].indirect(offsets))
+
+        w1_sb = [held([P, 2 * PASSES, 2 * H], U8, f"w1_sb{pair}") for pair in range(E // 2)]
+        for pair in range(E // 2):
+            if pair == LIFT_BEFORE:
+                for r in range(4):
+                    nc.sync.dma_start(out=lifted[:].bitcast(I32)[r:P:32], in_=stacked[:].bitcast(I32)[4 + r : P : 32])
+            experts = w1_words[2 * pair : 2 * pair + 2]
+            nc.sync.dma_start(out=w1_sb[pair][:].bitcast(I32), in_=experts.rearrange("e s p b -> p (e s) b").bitcast(I32))
+        token_lists = [keep.tile([P, T // PER_COLUMN], U16, name=f"token_list{r}") for r in range(2)]
         for r, pos in enumerate((pos1, pos2)):
             nc.sync.dma_start(token_lists[r][:], pos)
-            nc.sync.dma_start(out=gate_sb[0][r][:], in_=gate[r, :, :HALF])
-        for r in range(2):
-            nc.sync.dma_start(out=gate_sb[1][r][:], in_=gate[r, :, HALF:])
+        load_rows([nc.sync] * 4, w2_plane, w2_scales.rearrange("e s (q r) n -> r q (e s) n", r=4))
+        w2_sb = held([P, E, 2 * N], U8, "w2_sb")
+        nc.sync.dma_start(out=w2_sb[:].bitcast(I32), in_=w2_words.rearrange("e s p b -> p (e s) b").bitcast(I32))
+        gate_sb = held([P, 2, T], F32, "gate_sb")
+        nc.sync.dma_start(out=gate_sb[:], in_=gate.rearrange("r p t -> p r t"))
+        nc.sync.dma_start(out=w1s_sb[1][:], in_=w1s_rows[:, :, WIDTH:])
+        load_stacked(w2s_plane, w2s_scales, SHARED_FIRST)
         w2s_sb = held([P, SHARED_PASSES, N], I32, "w2s_sb")
         nc.sync.dma_start(out=w2s_sb[:], in_=w2s_words.rearrange("s p n d -> p s (n d)").bitcast(I32))
-        load_stacked(nc.sync, w2s_plane, w2s_scales, SHARED_FIRST)
 
         picked = {}
-        for lo, hi in GROUPS:
-            gather_words(lo, hi)
-            for e in range(lo, hi):
+        for lo in range(0, E, 2):
+            offsets = slot_list[:, lo * C // PER_COLUMN : (lo + 2) * C // PER_COLUMN]
+            words = [held([P, 2 * C], U32, f"words{lo}_{s}") for s in range(PASSES)]
+            for s in range(PASSES):
+                nc.vector.tensor_copy(words[s][:], x_sb[:, s, :].bitcast(U32).indirect(offsets))
+            for e in range(lo, lo + 2):
                 cols = slice((e - lo) * C, (e - lo + 1) * C)
-                picked[e] = [(words[lo, s][:, cols], plane[:, e * C : (e + 1) * C]) for s, plane in enumerate((stacked, lifted))]
+                picked[e] = [(words[s][:, cols], plane[:, e * C : (e + 1) * C]) for s, plane in enumerate((stacked, lifted))]
 
         banks = [psum.tile([P, WIDTH], F32, name=f"bank{b}") for b in range(8)]
 
-        def first_layer(unit, tokens, weights):
-            acc = banks[unit % SUM_BANKS]
+        def first_layer(acc, tokens, weights, name):
             for s in range(PASSES):
                 nc.tensor.matmul_mx(
                     out=acc[:], lhsT=tokens[s][0].bitcast(FP8X4), lhsT_scale=tokens[s][1],
                     rhs=weights[s][0], rhs_scale=weights[s][1], start=(s == 0), stop=(s == PASSES - 1),
                 )
-            hidden = held([P, WORDS], F32, f"hidden{unit}")
+            hidden = held([P, WORDS], F32, name)
             rounded = hidden[:].bitcast(BF16).rearrange("s (u p e) -> s u p e", u=2, e=2)
             sums = acc[:].rearrange("s (p u e) -> s u p e", u=2, e=2)
-            if unit == E - 1:
-                nc.vector.tensor_scalar_max(rounded, sums, 0.0)
-            else:
-                nc.scalar.activation(out=rounded, in_=sums, func=RELU)
+            nc.scalar.activation(out=rounded, in_=sums, func=RELU)
             return hidden
 
-        def turn_and_quantise(bank, hiddens, copy, name):
+        def turn(bank, hiddens, copy, grouped):
             count = len(hiddens)
             turned = bank[:, : count * WORDS].rearrange("p (j u s) -> p j u s", j=count, u=2)
             for j in reversed(range(count)):
                 for u in range(2):
                     nc.tensor.transpose(turned[:, j, u, :], hiddens[j][:, u * P : (u + 1) * P], ident[:])
-            grouped = held([P, count * WORDS], F32, f"grouped_{name}")
-            copy(out=grouped[:].rearrange("p (j s u) -> p j s u", j=count, u=2), in_=turned.rearrange("p j u s -> p j s u"))
-            codes = held([P, count * P], U32, f"codes_{name}")
-            plane = held([P, count * P], U8, f"plane_{name}")
-            nc.vector.quantize_mx(out=codes[:].bitcast(FP8X4), scales=plane[:], in_=grouped[:].bitcast(BF16))
-            return codes, plane
+            copy(out=grouped.rearrange("p (j s u) -> p j s u", j=count, u=2), in_=turned.rearrange("p j u s -> p j s u"))
 
-        def routed_sums(e):
-            plane = w1_early_plane if e < E // 2 else w1_late_plane
-            weights = [(w1_sb[e][:, s, :].bitcast(FP4X4), plane[:, e % (E // 2) * PASSES + s, :]) for s in range(PASSES)]
-            return first_layer(e, picked[e], weights)
+        def quantise(codes, plane, grouped):
+            nc.vector.quantize_mx(out=codes.bitcast(FP8X4), scales=plane, in_=grouped.bitcast(BF16))
 
-        hiddens, routed_codes = [], []
-        for i, (lo, hi) in enumerate(GROUPS):
-            hiddens.extend(routed_sums(e) for e in range(len(hiddens), min(hi + 2, E)))
-            copy = nc.vector.tensor_copy if i in SWAPPED else nc.scalar.copy
-            routed_codes.append(turn_and_quantise(banks[SUM_BANKS + i], hiddens[lo:hi], copy, f"h{i}"))
-
-        y_sb = [held([P, SLOTS], F32, f"y_sb{b}") for b in range(BLOCKS)]
-        for i, (lo, hi) in enumerate(GROUPS):
-            codes, plane = routed_codes[i]
-            results = banks[SUM_BANKS + i][:].rearrange("p (b j) -> p b j", b=BLOCKS)
-            for b in range(BLOCKS):
-                for e in range(lo, hi):
-                    cols = slice((e - lo) * C, (e - lo + 1) * C)
-                    nc.tensor.matmul_mx(
-                        out=results[:, b, cols],
-                        lhsT=w2_sb[e // (E // 2)][:, e % (E // 2), 2 * b * P : 2 * (b + 1) * P].bitcast(FP4X4),
-                        lhsT_scale=w2_plane[:, e, b * P : (b + 1) * P],
-                        rhs=codes[:, cols].bitcast(FP8X4), rhs_scale=plane[:, cols], start=True, stop=True,
-                    )
-            copy = nc.scalar.copy if i in SWAPPED else nc.vector.tensor_copy
-            for b in range(BLOCKS):
-                copy(y_sb[b][:, lo * C : hi * C], results[:, b, : (hi - lo) * C])
-
-        def shared_sums(index):
-            g, tile = index // 4, index % 4
+        def shared_sums(g, tile, acc):
             first = [SHARED_FIRST + 4 * s for s in range(PASSES)]
             weights = [(w1s_sb[g][:, s, :].bitcast(FP8X4), w1s_plane[first[s] :, g * WIDTH : (g + 1) * WIDTH]) for s in range(PASSES)]
             cols = slice(tile * P, (tile + 1) * P)
-            return first_layer(E + index, [(x_sb[s][:, cols], x_plane[4 * s :, cols]) for s in range(PASSES)], weights)
+            return first_layer(acc, [(x_sb[:, s, cols], x_plane[4 * s :, cols]) for s in range(PASSES)], weights, f"hs{g}_{tile}")
 
-        pairs = 2 * SHARED_PASSES
-        shared_hiddens, shared_codes = [], []
-        for pair in range(pairs):
-            shared_hiddens.extend(shared_sums(index) for index in range(len(shared_hiddens), min(2 * pair + 3, 2 * pairs)))
-            units = shared_hiddens[2 * pair : 2 * pair + 2]
-            shared_codes.append(turn_and_quantise(banks[SUM_BANKS + pair % 2], units, nc.scalar.copy, f"hs{pair}"))
+        def routed_sums(e):
+            weights = [(w1_sb[e // 2][:, e % 2 * PASSES + s, :].bitcast(FP4X4), w1_plane[:, e * PASSES + s, :]) for s in range(PASSES)]
+            return first_layer(banks[e % SUM_BANKS], picked[e], weights, f"h{e}")
 
-        shared_banks = [banks[5], banks[6], banks[7], banks[2]]
-        out_rows = out.rearrange("(b p) t -> p b t", p=P)
+        shared_codes = [held([P, T], U32, f"shared_codes{g}") for g in range(SHARED_PASSES)]
+        shared_planes = [held([P, T], U8, f"shared_plane{g}") for g in range(SHARED_PASSES)]
+
+        early = [shared_sums(0, tile, banks[tile]) for tile in range(TILES)]
+
+        hiddens, routed = [], {}
+        for i, (lo, hi) in enumerate(GROUPS):
+            hiddens.extend(routed_sums(e) for e in range(len(hiddens), min(len(hiddens) + SUM_BANKS, E)))
+            grouped = held([P, (hi - lo) * WORDS], F32, f"grouped{i}")
+            turn(banks[TURN_BANKS[i]], hiddens[lo:hi], nc.vector.tensor_copy if i in VECTOR_TURNS else nc.scalar.copy, grouped[:])
+            codes = held([P, (hi - lo) * C], U32, f"codes{i}")
+            plane = held([P, (hi - lo) * C], U8, f"plane{i}")
+            quantise(codes[:], plane[:], grouped[:])
+            for e in range(lo, hi):
+                cols = slice((e - lo) * C, (e - lo + 1) * C)
+                routed[e] = (codes[:, cols], plane[:, cols])
+
+        def second_layer(results, e, b):
+            nc.tensor.matmul_mx(
+                out=results,
+                lhsT=w2_sb[:, e, 2 * b * P : 2 * (b + 1) * P].bitcast(FP4X4), lhsT_scale=w2_plane[:, e, b * P : (b + 1) * P],
+                rhs=routed[e][0].bitcast(FP8X4), rhs_scale=routed[e][1], start=True, stop=True,
+            )
+
+        y_sb = [held([P, SLOTS], F32, f"y_sb{b}") for b in range(BLOCKS)]
+        for lo, hi, bank in RESULT_RUNS:
+            for b, copy in enumerate((nc.scalar.copy, nc.vector.tensor_copy)):
+                for e in range(lo, hi):
+                    second_layer(banks[bank + b][:, (e - lo) * C : (e - lo + 1) * C], e, b)
+                copy(y_sb[b][:, lo * C : hi * C], banks[bank + b][:, : (hi - lo) * C])
+        for b in range(BLOCKS):
+            second_layer(banks[7][:, b * C : (b + 1) * C], E - 1, b)
+        for b in range(BLOCKS):
+            nc.scalar.copy(y_sb[b][:, (E - 1) * C :], banks[7][:, b * C : (b + 1) * C])
+
+        early_grouped = held([P, TILES * WORDS], F32, "early_grouped")
+        for pair in range(2):
+            turn(banks[3 - pair], early[2 * pair : 2 * pair + 2], nc.scalar.copy, early_grouped[:, pair * WIDTH : (pair + 1) * WIDTH])
+        quantise(shared_codes[0][:], shared_planes[0][:], early_grouped[:])
+
+        late, late_grouped = [], []
+        for pair in range(2):
+            late.extend(shared_sums(1, tile, banks[(tile + 2) % SUM_BANKS]) for tile in range(len(late), min(2 * pair + 3, TILES)))
+            late_grouped.append(held([P, WIDTH], F32, f"late_grouped{pair}"))
+            turn(banks[4 + 3 * pair], late[2 * pair : 2 * pair + 2], nc.scalar.copy, late_grouped[pair][:])
+            cols = slice(pair * HALF, (pair + 1) * HALF)
+            quantise(shared_codes[1][:, cols], shared_planes[1][:, cols], late_grouped[pair][:])
+
+        shared = [banks[5 + half][:].rearrange("p (b t) -> p b t", b=BLOCKS) for half in range(2)]
         for half in range(2):
-            shared = [shared_banks[BLOCKS * half + b][:, :HALF] for b in range(BLOCKS)]
+            cols = slice(half * HALF, (half + 1) * HALF)
             for b in range(BLOCKS):
                 for g in range(SHARED_PASSES):
-                    codes, plane = shared_codes[2 * g + half]
                     nc.tensor.matmul_mx(
-                        out=shared[b],
-                        lhsT=w2s_sb[:, g, b * P : (b + 1) * P].bitcast(FP8X4),
-                        lhsT_scale=w2s_plane[SHARED_FIRST + 4 * g :, b * P : (b + 1) * P],
-                        rhs=codes[:].bitcast(FP8X4), rhs_scale=plane[:], start=(g == 0), stop=(g == SHARED_PASSES - 1),
+                        out=shared[half][:, b, :],
+                        lhsT=w2s_sb[:, g, b * P : (b + 1) * P].bitcast(FP8X4), lhsT_scale=w2s_plane[SHARED_FIRST + 4 * g :, b * P : (b + 1) * P],
+                        rhs=shared_codes[g][:, cols].bitcast(FP8X4), rhs_scale=shared_planes[g][:, cols], start=(g == 0), stop=(g == SHARED_PASSES - 1),
                     )
-            terms = []
+
+        both = [held([P, BLOCKS, HALF], F32, f"both{half}") for half in range(2)]
+        for b in range(BLOCKS):
+            terms = [early_grouped[:, :T], late_grouped[1][:]] if b == 1 else [held([P, T], F32, f"term{r}")[:] for r in range(2)]
             for r in range(2):
-                offsets = token_lists[r][:, half * HALF // PER_COLUMN : (half + 1) * HALF // PER_COLUMN]
-                if (half, r) == (1, 1):
-                    terms.append([shared_hiddens[2 * (pairs - BLOCKS + b) + 1] for b in range(BLOCKS)])
-                else:
-                    terms.append([held([P, HALF], F32, f"term{half}_{r}_{b}") for b in range(BLOCKS)])
-                for b in range(BLOCKS):
-                    nc.vector.tensor_tensor(terms[r][b][:], y_sb[b][:].indirect(offsets), gate_sb[half][r][:], MULT)
-            for b in range(BLOCKS):
-                routed = held([P, HALF], F32, f"routed{half}_{b}")
-                nc.vector.tensor_tensor(routed[:], terms[0][b][:], terms[1][b][:], ADD)
-                total = held([P, HALF], F32, f"total{half}_{b}")
-                nc.vector.tensor_tensor(total[:], shared[b], routed[:], ADD)
-                nc.sync.dma_start(out=out_rows[:, b, half * HALF : (half + 1) * HALF], in_=total[:])
+                nc.vector.tensor_tensor(terms[r], y_sb[b][:].indirect(token_lists[r][:]), gate_sb[:, r, :], MULT)
+            for half in range(2):
+                cols = slice(half * HALF, (half + 1) * HALF)
+                nc.vector.tensor_tensor(both[half][:, b, :], terms[0][:, cols], terms[1][:, cols], ADD)
+        out_rows = out.rearrange("(b p) t -> p b t", p=P)
+        for half, blocks in [(0, slice(0, BLOCKS))] + [(1, slice(b, b + 1)) for b in range(BLOCKS)]:
+            total = held([P, blocks.stop - blocks.start, HALF], F32, f"total{half}_{blocks.start}")
+            nc.vector.tensor_tensor(total[:], shared[half][:, blocks, :], both[half][:, blocks, :], ADD)
+            nc.sync.dma_start(out=out_rows[:, blocks, half * HALF : (half + 1) * HALF], in_=total[:])

@@ -14,6 +14,7 @@ U16 = mybir.dt.uint16
 U8 = mybir.dt.uint8
 FP8X4 = mybir.dt.float8_e4m3fn_x4
 FP4X4 = mybir.dt.float4_e2m1fn_x4
+COPY = mybir.ActivationFunctionType.Copy
 RELU = mybir.ActivationFunctionType.Relu
 MULT = mybir.AluOpType.mult
 ADD = mybir.AluOpType.add
@@ -101,9 +102,10 @@ def tile_moe_shf_mlp_relu_kernel(
         load_rows([nc.sync] * 4, w2_plane, w2_scales.rearrange("e s (q r) n -> r q (e s) n", r=4))
         w2_sb = held([P, E, 2 * N], U8, "w2_sb")
         nc.sync.dma_start(out=w2_sb[:].bitcast(I32), in_=w2_words.rearrange("e s p b -> p (e s) b").bitcast(I32))
-        gate_sb = held([P, 2, T], F32, "gate_sb")
-        nc.sync.dma_start(out=gate_sb[:], in_=gate.rearrange("r p t -> p r t"))
         nc.sync.dma_start(out=w1s_sb[1][:], in_=w1s_rows[:, :, WIDTH:])
+        gates = [held([P, T], F32, f"gate{r}") for r in range(2)]
+        for r in range(2):
+            nc.sync.dma_start(out=gates[r][:], in_=gate[r])
         load_stacked(w2s_plane, w2s_scales, SHARED_FIRST)
         w2s_sb = held([P, SHARED_PASSES, N], I32, "w2s_sb")
         nc.sync.dma_start(out=w2s_sb[:], in_=w2s_words.rearrange("s p n d -> p s (n d)").bitcast(I32))
@@ -120,14 +122,13 @@ def tile_moe_shf_mlp_relu_kernel(
 
         banks = [psum.tile([P, WIDTH], F32, name=f"bank{b}") for b in range(8)]
 
-        def first_layer(acc, tokens, weights, name):
+        def first_layer(acc, tokens, weights, hidden):
             for s in range(PASSES):
                 nc.tensor.matmul_mx(
                     out=acc[:], lhsT=tokens[s][0].bitcast(FP8X4), lhsT_scale=tokens[s][1],
                     rhs=weights[s][0], rhs_scale=weights[s][1], start=(s == 0), stop=(s == PASSES - 1),
                 )
-            hidden = held([P, WORDS], F32, name)
-            rounded = hidden[:].bitcast(BF16).rearrange("s (u p e) -> s u p e", u=2, e=2)
+            rounded = hidden.bitcast(BF16).rearrange("s (u p e) -> s u p e", u=2, e=2)
             sums = acc[:].rearrange("s (p u e) -> s u p e", u=2, e=2)
             nc.scalar.activation(out=rounded, in_=sums, func=RELU)
             return hidden
@@ -143,20 +144,20 @@ def tile_moe_shf_mlp_relu_kernel(
         def quantise(codes, plane, grouped):
             nc.vector.quantize_mx(out=codes.bitcast(FP8X4), scales=plane, in_=grouped.bitcast(BF16))
 
-        def shared_sums(g, tile, acc):
+        def shared_sums(g, tile, acc, hidden):
             first = [SHARED_FIRST + 4 * s for s in range(PASSES)]
             weights = [(w1s_sb[g][:, s, :].bitcast(FP8X4), w1s_plane[first[s] :, g * WIDTH : (g + 1) * WIDTH]) for s in range(PASSES)]
             cols = slice(tile * P, (tile + 1) * P)
-            return first_layer(acc, [(x_sb[:, s, cols], x_plane[4 * s :, cols]) for s in range(PASSES)], weights, f"hs{g}_{tile}")
+            return first_layer(acc, [(x_sb[:, s, cols], x_plane[4 * s :, cols]) for s in range(PASSES)], weights, hidden)
 
         def routed_sums(e):
             weights = [(w1_sb[e // 2][:, e % 2 * PASSES + s, :].bitcast(FP4X4), w1_plane[:, e * PASSES + s, :]) for s in range(PASSES)]
-            return first_layer(banks[e % SUM_BANKS], picked[e], weights, f"h{e}")
+            return first_layer(banks[e % SUM_BANKS], picked[e], weights, held([P, WORDS], F32, f"h{e}")[:])
 
-        shared_codes = [held([P, T], U32, f"shared_codes{g}") for g in range(SHARED_PASSES)]
+        shared_codes = [keep.tile([P, T], U32, name=f"shared_codes{g}", tag=f"shared_codes{g}", align_bytes=64) for g in range(SHARED_PASSES)]
         shared_planes = [held([P, T], U8, f"shared_plane{g}") for g in range(SHARED_PASSES)]
 
-        early = [shared_sums(0, tile, banks[tile]) for tile in range(TILES)]
+        early = [shared_sums(0, tile, banks[tile], held([P, WORDS], F32, f"hs{tile}")[:]) for tile in range(TILES)]
 
         hiddens, routed = [], {}
         for i, (lo, hi) in enumerate(GROUPS):
@@ -194,34 +195,41 @@ def tile_moe_shf_mlp_relu_kernel(
         quantise(shared_codes[0][:], shared_planes[0][:], early_grouped[:])
 
         late, late_grouped = [], []
+        late_hidden = [held([P, 2, WORDS], F32, f"late_hidden{pair}") for pair in range(2)]
         for pair in range(2):
-            late.extend(shared_sums(1, tile, banks[(tile + 2) % SUM_BANKS]) for tile in range(len(late), min(2 * pair + 3, TILES)))
+            late.extend(shared_sums(1, tile, banks[(tile + 2) % SUM_BANKS], late_hidden[tile // 2][:, tile % 2, :]) for tile in range(len(late), min(2 * pair + 3, TILES)))
             late_grouped.append(held([P, WIDTH], F32, f"late_grouped{pair}"))
             turn(banks[4 + 3 * pair], late[2 * pair : 2 * pair + 2], nc.scalar.copy, late_grouped[pair][:])
             cols = slice(pair * HALF, (pair + 1) * HALF)
             quantise(shared_codes[1][:, cols], shared_planes[1][:, cols], late_grouped[pair][:])
 
-        shared = [banks[5 + half][:].rearrange("p (b t) -> p b t", b=BLOCKS) for half in range(2)]
-        for half in range(2):
-            cols = slice(half * HALF, (half + 1) * HALF)
+        for g in range(SHARED_PASSES):
             for b in range(BLOCKS):
-                for g in range(SHARED_PASSES):
-                    nc.tensor.matmul_mx(
-                        out=shared[half][:, b, :],
-                        lhsT=w2s_sb[:, g, b * P : (b + 1) * P].bitcast(FP8X4), lhsT_scale=w2s_plane[SHARED_FIRST + 4 * g :, b * P : (b + 1) * P],
-                        rhs=shared_codes[g][:, cols].bitcast(FP8X4), rhs_scale=shared_planes[g][:, cols], start=(g == 0), stop=(g == SHARED_PASSES - 1),
-                    )
+                nc.tensor.matmul_mx(
+                    out=banks[5 + b][:],
+                    lhsT=w2s_sb[:, g, b * P : (b + 1) * P].bitcast(FP8X4), lhsT_scale=w2s_plane[SHARED_FIRST + 4 * g :, b * P : (b + 1) * P],
+                    rhs=shared_codes[g][:].bitcast(FP8X4), rhs_scale=shared_planes[g][:], start=(g == 0), stop=(g == SHARED_PASSES - 1),
+                )
 
-        both = [held([P, BLOCKS, HALF], F32, f"both{half}") for half in range(2)]
-        for b in range(BLOCKS):
-            terms = [early_grouped[:, :T], late_grouped[1][:]] if b == 1 else [held([P, T], F32, f"term{r}")[:] for r in range(2)]
-            for r in range(2):
-                nc.vector.tensor_tensor(terms[r], y_sb[b][:].indirect(token_lists[r][:]), gate_sb[:, r, :], MULT)
-            for half in range(2):
-                cols = slice(half * HALF, (half + 1) * HALF)
-                nc.vector.tensor_tensor(both[half][:, b, :], terms[0][:, cols], terms[1][:, cols], ADD)
+        def combined(name, left, right, op):
+            result = held([P, right.shape[1]], F32, name)
+            nc.vector.tensor_tensor(result[:], left, right, op)
+            return result
+
         out_rows = out.rearrange("(b p) t -> p b t", p=P)
-        for half, blocks in [(0, slice(0, BLOCKS))] + [(1, slice(b, b + 1)) for b in range(BLOCKS)]:
-            total = held([P, blocks.stop - blocks.start, HALF], F32, f"total{half}_{blocks.start}")
-            nc.vector.tensor_tensor(total[:], shared[half][:, blocks, :], both[half][:, blocks, :], ADD)
-            nc.sync.dma_start(out=out_rows[:, blocks, half * HALF : (half + 1) * HALF], in_=total[:])
+        terms = [combined(f"term{r}", y_sb[0][:].indirect(token_lists[r][:]), gates[r][:], MULT) for r in range(2)]
+        columns = [hidden[:].rearrange("p j w -> p (j w)") for hidden in late_hidden]
+        for r in range(2):
+            nc.scalar.activation(columns[r], y_sb[1][:].indirect(token_lists[r][:]), COPY)
+        both = combined("both", terms[0][:], terms[1][:], ADD)
+        other = combined("other", columns[0], gates[0][:], MULT)
+        total = combined("total", banks[5][:], both[:], ADD)
+        nc.sync.dma_start(out=out_rows[:, 0, :], in_=total[:])
+        part = combined("part", banks[6][:], other[:], ADD)
+        halves = [slice(half * HALF, (half + 1) * HALF) for half in range(2)]
+        last = keep.tile([P, T], F32, name="last", tag="shared_codes1", align_bytes=64)
+        for cols in halves:
+            nc.vector.tensor_tensor(last[:, cols], columns[1][:, cols], gates[1][:, cols], MULT)
+        for half, cols in enumerate(halves):
+            total = combined(f"total{half}", part[:, cols], last[:, cols], ADD)
+            nc.sync.dma_start(out=out_rows[:, 1, cols], in_=total[:])

@@ -22,6 +22,7 @@ ADD = mybir.AluOpType.add
 P = 128
 WIDTH = 512
 WORDS = WIDTH // 2
+PACK = 4
 PASSES = K // WIDTH
 SHARED_PASSES = HS // WIDTH
 BLOCKS = N // P
@@ -30,12 +31,9 @@ TILES = T // P
 HALF = T // 2
 PER_COLUMN = 16
 GROUPS = [(0, 2), (2, 4), (4, 6), (6, 7), (7, 8)]
-SUM_BANKS = 4
-TURN_BANKS = (4, 2, 6, 7, 4)
-VECTOR_TURNS = (1, 3)
-RESULT_RUNS = [(0, 4, 0), (4, 7, 5)]
-SHARED_FIRST = 8
-LIFT_BEFORE = 1
+EARLY = 4
+W1S_FIRST = 4
+W2S_FIRST = 8
 
 
 def tile_moe_shf_mlp_relu_kernel(
@@ -54,9 +52,9 @@ def tile_moe_shf_mlp_relu_kernel(
             engine.memset(plane[:].bitcast(I32), 0)
             return plane
 
-        def load_rows(queues, plane, rows):
-            for r, queue in enumerate(queues):
-                queue.dma_start(out=plane[:].bitcast(I32)[r:P:32], in_=rows[r].bitcast(I32))
+        def load_rows(plane, rows):
+            for r in range(4):
+                nc.sync.dma_start(out=plane[:].bitcast(I32)[r:P:32], in_=rows[r].bitcast(I32))
 
         def load_stacked(plane, scales, first):
             for q in range(4):
@@ -65,48 +63,67 @@ def tile_moe_shf_mlp_relu_kernel(
                 )
 
         x_plane = zeroed_plane([P, T], "x_plane", nc.gpsimd)
+        w1s_loaded_plane = zeroed_plane([P, HS], "w1s_loaded_plane", nc.gpsimd)
         w1_plane = zeroed_plane([P, E * PASSES, H], "w1_plane", nc.vector)
-        w1s_plane = zeroed_plane([P, HS], "w1s_plane", nc.vector)
-        lifted = zeroed_plane([P, SLOTS], "lifted", nc.vector)
-        w2_plane = zeroed_plane([P, E, N], "w2_plane", nc.vector)
-        w2s_plane = zeroed_plane([P, N], "w2s_plane", nc.vector)
+        lifted = zeroed_plane([P, SLOTS], "lifted", nc.gpsimd)
+        w2s_plane = zeroed_plane([P, N], "w2s_plane", nc.gpsimd)
         ident = held([P, P], F32, "ident")
         make_identity(nc, ident[:])
+        w2_plane = zeroed_plane([P, E, N], "w2_plane", nc.gpsimd)
 
         slot_list = keep.tile([P, SLOTS // PER_COLUMN], U16, name="slot_list")
+        nc.sync.dma_start(slot_list[:], offs)
+        load_stacked(x_plane, x_scales, 0)
+        w1s_loaded = [held([P, PASSES, WIDTH], I32, f"w1s_loaded{g}") for g in range(SHARED_PASSES)]
+        w1s_rows = w1s_words.rearrange("s p l d -> p s (l d)").bitcast(I32)
+        nc.sync.dma_start(out=w1s_loaded[0][:], in_=w1s_rows[:, :, :WIDTH])
+        load_stacked(w1s_loaded_plane, w1s_scales, W1S_FIRST)
         x_sb = held([P, PASSES, T], I32, "x_sb")
         nc.sync.dma_start(out=x_sb[:], in_=x_words.rearrange("s p t d -> p s (t d)").bitcast(I32))
-        load_stacked(x_plane, x_scales, 0)
-        nc.sync.dma_start(slot_list[:], offs)
-        w1s_sb = [held([P, PASSES, WIDTH], I32, f"w1s_sb{g}") for g in range(SHARED_PASSES)]
-        w1s_rows = w1s_words.rearrange("s p l d -> p s (l d)").bitcast(I32)
-        nc.sync.dma_start(out=w1s_sb[0][:], in_=w1s_rows[:, :, :WIDTH])
-        load_stacked(w1s_plane, w1s_scales, SHARED_FIRST)
-        load_rows([nc.gpsimd, nc.gpsimd, nc.sync, nc.sync], w1_plane, w1_scales.rearrange("e s (q r) i -> r q (e s) i", r=4))
+        load_rows(w1_plane, w1_scales.rearrange("e s (q r) i -> r q (e s) i", r=4))
 
         stacked = held([P, SLOTS], U8, "stacked")
         for lo in range(0, SLOTS, 2 * C):
             offsets = slot_list[:, lo // PER_COLUMN : (lo + 2 * C) // PER_COLUMN]
             nc.vector.tensor_copy(stacked[:, lo : lo + 2 * C], x_plane[:].indirect(offsets))
 
+        w1s_sb = [keep.tile([P, PASSES, WIDTH], U32, name=f"w1s_sb{g}", tag=f"w1s_sb{g}", align_bytes=64) for g in range(SHARED_PASSES)]
+        w1s_planes = {}
+
+        def permute_plane(g):
+            w1s_planes[g] = keep.tile([P, WIDTH], U8, name=f"w1s_plane{g}", tag="w1s_plane", align_bytes=64)
+            nc.gpsimd.tensor_copy(
+                out=w1s_planes[g][:].rearrange("p (t m) -> p t m", t=PACK),
+                in_=w1s_loaded_plane[:, g * WIDTH : (g + 1) * WIDTH].rearrange("p (m t) -> p t m", t=PACK),
+            )
+
+        def permute_words(g, copy):
+            for s in range(PASSES):
+                copy(
+                    out=w1s_sb[g][:, s, :].rearrange("p (t b i) -> p b t i", t=PACK, i=PACK),
+                    in_=w1s_loaded[g][:, s, :].bitcast(U32).rearrange("p (b i t) -> p b t i", t=PACK, i=PACK),
+                )
+
+        permute_plane(0)
+        permute_words(0, nc.scalar.copy)
+
         w1_sb = [held([P, 2 * PASSES, 2 * H], U8, f"w1_sb{pair}") for pair in range(E // 2)]
         for pair in range(E // 2):
-            if pair == LIFT_BEFORE:
+            if pair == 1:
                 for r in range(4):
                     nc.sync.dma_start(out=lifted[:].bitcast(I32)[r:P:32], in_=stacked[:].bitcast(I32)[4 + r : P : 32])
             experts = w1_words[2 * pair : 2 * pair + 2]
             nc.sync.dma_start(out=w1_sb[pair][:].bitcast(I32), in_=experts.rearrange("e s p b -> p (e s) b").bitcast(I32))
-        token_lists = [keep.tile([P, T // PER_COLUMN], U16, name=f"token_list{r}") for r in range(2)]
-        for r, pos in enumerate((pos1, pos2)):
-            nc.sync.dma_start(token_lists[r][:], pos)
-        load_rows([nc.sync] * 4, w2_plane, w2_scales.rearrange("e s (q r) n -> r q (e s) n", r=4))
+        load_rows(w2_plane, w2_scales.rearrange("e s (q r) n -> r q (e s) n", r=4))
         w2_sb = held([P, E, 2 * N], U8, "w2_sb")
         nc.sync.dma_start(out=w2_sb[:].bitcast(I32), in_=w2_words.rearrange("e s p b -> p (e s) b").bitcast(I32))
-        nc.sync.dma_start(out=w1s_sb[1][:], in_=w1s_rows[:, :, WIDTH:])
+        nc.sync.dma_start(out=w1s_loaded[1][:], in_=w1s_rows[:, :, WIDTH:])
+        token_lists = [keep.tile([P, T // PER_COLUMN], U16, name=f"token_list{r}") for r in range(2)]
         gates = [held([P, T], F32, f"gate{r}") for r in range(2)]
-        for r in range(2):
+        for r, pos in enumerate((pos1, pos2)):
+            nc.sync.dma_start(token_lists[r][:], pos)
             nc.sync.dma_start(out=gates[r][:], in_=gate[r])
-        load_stacked(w2s_plane, w2s_scales, SHARED_FIRST)
+        load_stacked(w2s_plane, w2s_scales, W2S_FIRST)
         w2s_sb = held([P, SHARED_PASSES, N], I32, "w2s_sb")
         nc.sync.dma_start(out=w2s_sb[:], in_=w2s_words.rearrange("s p n d -> p s (n d)").bitcast(I32))
 
@@ -122,92 +139,106 @@ def tile_moe_shf_mlp_relu_kernel(
 
         banks = [psum.tile([P, WIDTH], F32, name=f"bank{b}") for b in range(8)]
 
-        def first_layer(acc, tokens, weights, hidden):
-            for s in range(PASSES):
-                nc.tensor.matmul_mx(
-                    out=acc[:], lhsT=tokens[s][0].bitcast(FP8X4), lhsT_scale=tokens[s][1],
-                    rhs=weights[s][0], rhs_scale=weights[s][1], start=(s == 0), stop=(s == PASSES - 1),
-                )
-            rounded = hidden.bitcast(BF16).rearrange("s (u p e) -> s u p e", u=2, e=2)
-            sums = acc[:].rearrange("s (p u e) -> s u p e", u=2, e=2)
-            nc.scalar.activation(out=rounded, in_=sums, func=RELU)
-            return hidden
-
-        def turn(bank, hiddens, copy, grouped):
-            count = len(hiddens)
-            turned = bank[:, : count * WORDS].rearrange("p (j u s) -> p j u s", j=count, u=2)
-            for j in reversed(range(count)):
-                for u in range(2):
-                    nc.tensor.transpose(turned[:, j, u, :], hiddens[j][:, u * P : (u + 1) * P], ident[:])
-            copy(out=grouped.rearrange("p (j s u) -> p j s u", j=count, u=2), in_=turned.rearrange("p j u s -> p j s u"))
-
-        def quantise(codes, plane, grouped):
-            nc.vector.quantize_mx(out=codes.bitcast(FP8X4), scales=plane, in_=grouped.bitcast(BF16))
-
-        def shared_sums(g, tile, acc, hidden):
-            first = [SHARED_FIRST + 4 * s for s in range(PASSES)]
-            weights = [(w1s_sb[g][:, s, :].bitcast(FP8X4), w1s_plane[first[s] :, g * WIDTH : (g + 1) * WIDTH]) for s in range(PASSES)]
-            cols = slice(tile * P, (tile + 1) * P)
-            return first_layer(acc, [(x_sb[:, s, cols], x_plane[4 * s :, cols]) for s in range(PASSES)], weights, hidden)
-
-        def routed_sums(e):
-            weights = [(w1_sb[e // 2][:, e % 2 * PASSES + s, :].bitcast(FP4X4), w1_plane[:, e * PASSES + s, :]) for s in range(PASSES)]
-            return first_layer(banks[e % SUM_BANKS], picked[e], weights, held([P, WORDS], F32, f"h{e}")[:])
-
+        shared_grouped = [[keep.tile([P, 2 * WIDTH], BF16, name=f"shared_grouped{g}_{pair}", tag=f"shared_grouped{g}_{pair}", align_bytes=64) for pair in range(2)] for g in range(SHARED_PASSES)]
         shared_codes = [keep.tile([P, T], U32, name=f"shared_codes{g}", tag=f"shared_codes{g}", align_bytes=64) for g in range(SHARED_PASSES)]
         shared_planes = [held([P, T], U8, f"shared_plane{g}") for g in range(SHARED_PASSES)]
 
-        early = [shared_sums(0, tile, banks[tile], held([P, WORDS], F32, f"hs{tile}")[:]) for tile in range(TILES)]
+        def shared_unit(g, tile, bank):
+            cols = slice(tile * P, (tile + 1) * P)
+            for t in range(PACK):
+                features = slice(t * P, (t + 1) * P)
+                for s in range(PASSES):
+                    nc.tensor.matmul_mx(
+                        out=bank[:, features],
+                        lhsT=w1s_sb[g][:, s, features].bitcast(FP8X4), lhsT_scale=w1s_planes[g][W1S_FIRST + 4 * s :, features],
+                        rhs=x_sb[:, s, cols].bitcast(FP8X4), rhs_scale=x_plane[4 * s :, cols], start=(s == 0), stop=(s == PASSES - 1),
+                    )
+            rounded = shared_grouped[g][tile // 2][:, tile % 2 * WIDTH : (tile % 2 + 1) * WIDTH]
+            nc.scalar.activation(out=rounded.rearrange("p (k t) -> p k t", t=PACK), in_=bank[:].rearrange("p (t k) -> p k t", t=PACK), func=RELU)
 
-        hiddens, routed = [], {}
-        for i, (lo, hi) in enumerate(GROUPS):
-            hiddens.extend(routed_sums(e) for e in range(len(hiddens), min(len(hiddens) + SUM_BANKS, E)))
-            grouped = held([P, (hi - lo) * WORDS], F32, f"grouped{i}")
-            turn(banks[TURN_BANKS[i]], hiddens[lo:hi], nc.vector.tensor_copy if i in VECTOR_TURNS else nc.scalar.copy, grouped[:])
-            codes = held([P, (hi - lo) * C], U32, f"codes{i}")
-            plane = held([P, (hi - lo) * C], U8, f"plane{i}")
-            quantise(codes[:], plane[:], grouped[:])
+        def quantise(codes, plane, grouped):
+            nc.vector.quantize_mx(out=codes.bitcast(FP8X4), scales=plane, in_=grouped)
+
+        def quantise_shared(g, pair):
+            cols = slice(pair * HALF, (pair + 1) * HALF)
+            quantise(shared_codes[g][:, cols], shared_planes[g][:, cols], shared_grouped[g][pair][:])
+
+        hiddens = [held([P, WORDS], F32, f"h{e}") for e in range(E)]
+
+        def routed_unit(e, bank):
+            for s in range(PASSES):
+                nc.tensor.matmul_mx(
+                    out=bank[:], lhsT=picked[e][s][0].bitcast(FP8X4), lhsT_scale=picked[e][s][1],
+                    rhs=w1_sb[e // 2][:, e % 2 * PASSES + s, :].bitcast(FP4X4), rhs_scale=w1_plane[:, e * PASSES + s, :],
+                    start=(s == 0), stop=(s == PASSES - 1),
+                )
+            rounded = hiddens[e][:].bitcast(BF16).rearrange("s (u p e) -> s u p e", u=2, e=2)
+            nc.scalar.activation(out=rounded, in_=bank[:].rearrange("s (p u e) -> s u p e", u=2, e=2), func=RELU)
+
+        routed = {}
+
+        def turn(i, bank, copy):
+            lo, hi = GROUPS[i]
+            count = hi - lo
+            turned = bank[:, : count * WORDS].rearrange("p (j u s) -> p j u s", j=count, u=2)
+            for j in reversed(range(count)):
+                for u in range(2):
+                    nc.tensor.transpose(turned[:, j, u, :], hiddens[lo + j][:, u * P : (u + 1) * P], ident[:])
+            grouped = held([P, count * WORDS], F32, f"grouped{i}")
+            copy(out=grouped[:].rearrange("p (j s u) -> p j s u", j=count, u=2), in_=turned.rearrange("p j u s -> p j s u"))
+            codes = held([P, count * C], U32, f"codes{i}")
+            plane = held([P, count * C], U8, f"plane{i}")
+            quantise(codes[:], plane[:], grouped[:].bitcast(BF16))
             for e in range(lo, hi):
                 cols = slice((e - lo) * C, (e - lo + 1) * C)
                 routed[e] = (codes[:, cols], plane[:, cols])
 
-        def second_layer(results, e, b):
-            nc.tensor.matmul_mx(
-                out=results,
-                lhsT=w2_sb[:, e, 2 * b * P : 2 * (b + 1) * P].bitcast(FP4X4), lhsT_scale=w2_plane[:, e, b * P : (b + 1) * P],
-                rhs=routed[e][0].bitcast(FP8X4), rhs_scale=routed[e][1], start=True, stop=True,
-            )
+        y_sb = held([P, BLOCKS, SLOTS], F32, "y_sb")
 
-        y_sb = [held([P, SLOTS], F32, f"y_sb{b}") for b in range(BLOCKS)]
-        for lo, hi, bank in RESULT_RUNS:
-            for b, copy in enumerate((nc.scalar.copy, nc.vector.tensor_copy)):
-                for e in range(lo, hi):
-                    second_layer(banks[bank + b][:, (e - lo) * C : (e - lo + 1) * C], e, b)
-                copy(y_sb[b][:, lo * C : hi * C], banks[bank + b][:, : (hi - lo) * C])
-        for b in range(BLOCKS):
-            second_layer(banks[7][:, b * C : (b + 1) * C], E - 1, b)
-        for b in range(BLOCKS):
-            nc.scalar.copy(y_sb[b][:, (E - 1) * C :], banks[7][:, b * C : (b + 1) * C])
+        def second_layer(i, bank, copy):
+            lo, hi = GROUPS[i]
+            results = bank[:, : BLOCKS * (hi - lo) * C].rearrange("p (b j) -> p b j", b=BLOCKS)
+            for e in range(lo, hi):
+                for b in range(BLOCKS):
+                    nc.tensor.matmul_mx(
+                        out=results[:, b, (e - lo) * C : (e - lo + 1) * C],
+                        lhsT=w2_sb[:, e, 2 * b * P : 2 * (b + 1) * P].bitcast(FP4X4), lhsT_scale=w2_plane[:, e, b * P : (b + 1) * P],
+                        rhs=routed[e][0].bitcast(FP8X4), rhs_scale=routed[e][1], start=True, stop=True,
+                    )
+            copy(out=y_sb[:, :, lo * C : hi * C], in_=results)
 
-        early_grouped = held([P, TILES * WORDS], F32, "early_grouped")
-        for pair in range(2):
-            turn(banks[3 - pair], early[2 * pair : 2 * pair + 2], nc.scalar.copy, early_grouped[:, pair * WIDTH : (pair + 1) * WIDTH])
-        quantise(shared_codes[0][:], shared_planes[0][:], early_grouped[:])
-
-        late, late_grouped = [], []
-        late_hidden = [held([P, 2, WORDS], F32, f"late_hidden{pair}") for pair in range(2)]
-        for pair in range(2):
-            late.extend(shared_sums(1, tile, banks[(tile + 2) % SUM_BANKS], late_hidden[tile // 2][:, tile % 2, :]) for tile in range(len(late), min(2 * pair + 3, TILES)))
-            late_grouped.append(held([P, WIDTH], F32, f"late_grouped{pair}"))
-            turn(banks[4 + 3 * pair], late[2 * pair : 2 * pair + 2], nc.scalar.copy, late_grouped[pair][:])
-            cols = slice(pair * HALF, (pair + 1) * HALF)
-            quantise(shared_codes[1][:, cols], shared_planes[1][:, cols], late_grouped[pair][:])
+        for tile in range(EARLY):
+            shared_unit(0, tile, banks[tile])
+        for e in range(4):
+            routed_unit(e, banks[(e + EARLY) % 4])
+        quantise_shared(0, 0)
+        quantise_shared(0, 1)
+        turn(0, banks[4], nc.vector.tensor_copy)
+        for e in range(4, 6):
+            routed_unit(e, banks[(e + EARLY) % 4])
+        turn(1, banks[5], nc.vector.tensor_copy)
+        for e in range(6, 8):
+            routed_unit(e, banks[(e + EARLY) % 4])
+        turn(2, banks[4], nc.vector.tensor_copy)
+        turn(3, banks[5], nc.vector.tensor_copy)
+        turn(4, banks[0], nc.scalar.copy)
+        second_layer(0, banks[6], nc.scalar.copy)
+        second_layer(1, banks[7], nc.vector.tensor_copy)
+        second_layer(2, banks[4], nc.scalar.copy)
+        second_layer(3, banks[5], nc.vector.tensor_copy)
+        second_layer(4, banks[0], nc.scalar.copy)
+        permute_plane(1)
+        permute_words(1, nc.gpsimd.tensor_copy)
+        for tile, bank in enumerate((1, 2, 3, 6)):
+            shared_unit(1, tile, banks[bank])
+            if tile % 2:
+                quantise_shared(1, tile // 2)
 
         for g in range(SHARED_PASSES):
-            for b in range(BLOCKS):
+            for b, bank in enumerate((7, 4)):
                 nc.tensor.matmul_mx(
-                    out=banks[5 + b][:],
-                    lhsT=w2s_sb[:, g, b * P : (b + 1) * P].bitcast(FP8X4), lhsT_scale=w2s_plane[SHARED_FIRST + 4 * g :, b * P : (b + 1) * P],
+                    out=banks[bank][:],
+                    lhsT=w2s_sb[:, g, b * P : (b + 1) * P].bitcast(FP8X4), lhsT_scale=w2s_plane[W2S_FIRST + 4 * g :, b * P : (b + 1) * P],
                     rhs=shared_codes[g][:].bitcast(FP8X4), rhs_scale=shared_planes[g][:], start=(g == 0), stop=(g == SHARED_PASSES - 1),
                 )
 
@@ -217,15 +248,19 @@ def tile_moe_shf_mlp_relu_kernel(
             return result
 
         out_rows = out.rearrange("(b p) t -> p b t", p=P)
-        terms = [combined(f"term{r}", y_sb[0][:].indirect(token_lists[r][:]), gates[r][:], MULT) for r in range(2)]
-        columns = [hidden[:].rearrange("p j w -> p (j w)") for hidden in late_hidden]
+        window = y_sb[:].rearrange("p b j -> p (b j)")
+        terms = [held([P, T], F32, "term0"), held([P, T], F32, "term1")]
         for r in range(2):
-            nc.scalar.activation(columns[r], y_sb[1][:].indirect(token_lists[r][:]), COPY)
+            nc.vector.tensor_tensor(terms[r][:], window.indirect(token_lists[r][:]), gates[r][:], MULT)
+        fetched = keep.tile([P, 2, T], F32, name="fetched", tag="w1s_sb1", align_bytes=64)
+        columns = [fetched[:, r, :] for r in range(2)]
+        for r in range(2):
+            nc.scalar.activation(columns[r], y_sb[:, 1, :].indirect(token_lists[r][:]), COPY)
         both = combined("both", terms[0][:], terms[1][:], ADD)
         other = combined("other", columns[0], gates[0][:], MULT)
-        total = combined("total", banks[5][:], both[:], ADD)
+        total = combined("total", banks[7][:], both[:], ADD)
         nc.sync.dma_start(out=out_rows[:, 0, :], in_=total[:])
-        part = combined("part", banks[6][:], other[:], ADD)
+        part = combined("part", banks[4][:], other[:], ADD)
         halves = [slice(half * HALF, (half + 1) * HALF) for half in range(2)]
         last = keep.tile([P, T], F32, name="last", tag="shared_codes1", align_bytes=64)
         for cols in halves:

@@ -114,10 +114,10 @@ def tile_moe_shf_mlp_relu_kernel(
                     nc.sync.dma_start(out=lifted[:].bitcast(I32)[r:P:32], in_=stacked[:].bitcast(I32)[4 + r : P : 32])
             experts = w1_words[2 * pair : 2 * pair + 2]
             nc.sync.dma_start(out=w1_sb[pair][:].bitcast(I32), in_=experts.rearrange("e s p b -> p (e s) b").bitcast(I32))
+        nc.sync.dma_start(out=w1s_loaded[1][:], in_=w1s_rows[:, :, WIDTH:])
         load_rows(w2_plane, w2_scales.rearrange("e s (q r) n -> r q (e s) n", r=4))
         w2_sb = held([P, E, 2 * N], U8, "w2_sb")
         nc.sync.dma_start(out=w2_sb[:].bitcast(I32), in_=w2_words.rearrange("e s p b -> p (e s) b").bitcast(I32))
-        nc.sync.dma_start(out=w1s_loaded[1][:], in_=w1s_rows[:, :, WIDTH:])
         token_lists = [keep.tile([P, T // PER_COLUMN], U16, name=f"token_list{r}") for r in range(2)]
         gates = [held([P, T], F32, f"gate{r}") for r in range(2)]
         for r, pos in enumerate((pos1, pos2)):
@@ -193,19 +193,16 @@ def tile_moe_shf_mlp_relu_kernel(
                 cols = slice((e - lo) * C, (e - lo + 1) * C)
                 routed[e] = (codes[:, cols], plane[:, cols])
 
-        y_sb = held([P, BLOCKS, SLOTS], F32, "y_sb")
+        y_sb = [held([P, SLOTS], F32, f"y_sb{b}") for b in range(BLOCKS)]
 
-        def second_layer(i, bank, copy):
-            lo, hi = GROUPS[i]
-            results = bank[:, : BLOCKS * (hi - lo) * C].rearrange("p (b j) -> p b j", b=BLOCKS)
+        def second_layer(b, lo, hi, results, copy):
             for e in range(lo, hi):
-                for b in range(BLOCKS):
-                    nc.tensor.matmul_mx(
-                        out=results[:, b, (e - lo) * C : (e - lo + 1) * C],
-                        lhsT=w2_sb[:, e, 2 * b * P : 2 * (b + 1) * P].bitcast(FP4X4), lhsT_scale=w2_plane[:, e, b * P : (b + 1) * P],
-                        rhs=routed[e][0].bitcast(FP8X4), rhs_scale=routed[e][1], start=True, stop=True,
-                    )
-            copy(out=y_sb[:, :, lo * C : hi * C], in_=results)
+                nc.tensor.matmul_mx(
+                    out=results[:, (e - lo) * C : (e - lo + 1) * C],
+                    lhsT=w2_sb[:, e, 2 * b * P : 2 * (b + 1) * P].bitcast(FP4X4), lhsT_scale=w2_plane[:, e, b * P : (b + 1) * P],
+                    rhs=routed[e][0].bitcast(FP8X4), rhs_scale=routed[e][1], start=True, stop=True,
+                )
+            copy(out=y_sb[b][:, lo * C : hi * C], in_=results[:, : (hi - lo) * C])
 
         for tile in range(EARLY):
             shared_unit(0, tile, banks[tile])
@@ -222,20 +219,20 @@ def tile_moe_shf_mlp_relu_kernel(
         turn(2, banks[4], nc.vector.tensor_copy)
         turn(3, banks[5], nc.vector.tensor_copy)
         turn(4, banks[0], nc.scalar.copy)
-        second_layer(0, banks[6], nc.scalar.copy)
-        second_layer(1, banks[7], nc.vector.tensor_copy)
-        second_layer(2, banks[4], nc.scalar.copy)
-        second_layer(3, banks[5], nc.vector.tensor_copy)
-        second_layer(4, banks[0], nc.scalar.copy)
+        second_layer(0, 0, 4, banks[6], nc.scalar.copy)
+        second_layer(0, 4, 7, banks[7], nc.vector.tensor_copy)
+        second_layer(0, 7, 8, banks[0], nc.vector.tensor_copy)
+        second_layer(1, 0, 4, banks[4], nc.scalar.copy)
+        second_layer(1, 4, 8, banks[5], nc.scalar.copy)
         permute_plane(1)
-        permute_words(1, nc.gpsimd.tensor_copy)
-        for tile, bank in enumerate((1, 2, 3, 6)):
+        permute_words(1, nc.vector.tensor_copy)
+        for tile, bank in enumerate((6, 7, 0, 4)):
             shared_unit(1, tile, banks[bank])
             if tile % 2:
                 quantise_shared(1, tile // 2)
 
         for g in range(SHARED_PASSES):
-            for b, bank in enumerate((7, 4)):
+            for b, bank in enumerate((1, 2)):
                 nc.tensor.matmul_mx(
                     out=banks[bank][:],
                     lhsT=w2s_sb[:, g, b * P : (b + 1) * P].bitcast(FP8X4), lhsT_scale=w2s_plane[W2S_FIRST + 4 * g :, b * P : (b + 1) * P],
@@ -248,19 +245,18 @@ def tile_moe_shf_mlp_relu_kernel(
             return result
 
         out_rows = out.rearrange("(b p) t -> p b t", p=P)
-        window = y_sb[:].rearrange("p b j -> p (b j)")
         terms = [held([P, T], F32, "term0"), held([P, T], F32, "term1")]
         for r in range(2):
-            nc.vector.tensor_tensor(terms[r][:], window.indirect(token_lists[r][:]), gates[r][:], MULT)
+            nc.vector.tensor_tensor(terms[r][:], y_sb[0][:].indirect(token_lists[r][:]), gates[r][:], MULT)
         fetched = keep.tile([P, 2, T], F32, name="fetched", tag="w1s_sb1", align_bytes=64)
         columns = [fetched[:, r, :] for r in range(2)]
         for r in range(2):
-            nc.scalar.activation(columns[r], y_sb[:, 1, :].indirect(token_lists[r][:]), COPY)
+            nc.scalar.activation(columns[r], y_sb[1][:].indirect(token_lists[r][:]), COPY)
         both = combined("both", terms[0][:], terms[1][:], ADD)
         other = combined("other", columns[0], gates[0][:], MULT)
-        total = combined("total", banks[7][:], both[:], ADD)
+        total = combined("total", banks[1][:], both[:], ADD)
         nc.sync.dma_start(out=out_rows[:, 0, :], in_=total[:])
-        part = combined("part", banks[4][:], other[:], ADD)
+        part = combined("part", banks[2][:], other[:], ADD)
         halves = [slice(half * HALF, (half + 1) * HALF) for half in range(2)]
         last = keep.tile([P, T], F32, name="last", tag="shared_codes1", align_bytes=64)
         for cols in halves:

@@ -32,6 +32,7 @@ HALF = T // 2
 PER_COLUMN = 16
 GROUPS = [(0, 2), (2, 4), (4, 6), (6, 7), (7, 8)]
 EARLY = 4
+WARM_UPS = 3
 W1S_FIRST = 4
 W2S_FIRST = 8
 
@@ -64,7 +65,7 @@ def tile_moe_shf_mlp_relu_kernel(
 
         x_plane = zeroed_plane([P, T], "x_plane", nc.gpsimd)
         w1s_loaded_plane = zeroed_plane([P, HS], "w1s_loaded_plane", nc.gpsimd)
-        w1_plane = zeroed_plane([P, E * PASSES, H], "w1_plane", nc.vector)
+        w1_planes = [zeroed_plane([P, E // 2 * PASSES, H], f"w1_plane{half}", nc.vector) for half in range(2)]
         lifted = zeroed_plane([P, SLOTS], "lifted", nc.gpsimd)
         w2s_plane = zeroed_plane([P, N], "w2s_plane", nc.gpsimd)
         ident = held([P, P], F32, "ident")
@@ -77,10 +78,16 @@ def tile_moe_shf_mlp_relu_kernel(
         w1s_loaded = [held([P, PASSES, WIDTH], I32, f"w1s_loaded{g}") for g in range(SHARED_PASSES)]
         w1s_rows = w1s_words.rearrange("s p l d -> p s (l d)").bitcast(I32)
         nc.sync.dma_start(out=w1s_loaded[0][:], in_=w1s_rows[:, :, :WIDTH])
+        banks = [psum.tile([P, WIDTH], F32, name=f"bank{b}") for b in range(8)]
+        stand_in = w1s_loaded[0][:, 1, :].bitcast(U8)
+        for j in range(WARM_UPS):
+            nc.tensor.matmul_mx(
+                out=banks[7][:], lhsT=w1s_loaded[0][:, 0, :P].bitcast(FP8X4), lhsT_scale=stand_in[:, :P],
+                rhs=w1s_loaded[0][:, 0, :].bitcast(FP8X4), rhs_scale=stand_in[:, :WIDTH], start=True, stop=True,
+            )
         load_stacked(w1s_loaded_plane, w1s_scales, W1S_FIRST)
         x_sb = held([P, PASSES, T], I32, "x_sb")
         nc.sync.dma_start(out=x_sb[:], in_=x_words.rearrange("s p t d -> p s (t d)").bitcast(I32))
-        load_rows(w1_plane, w1_scales.rearrange("e s (q r) i -> r q (e s) i", r=4))
 
         stacked = held([P, SLOTS], U8, "stacked")
         for lo in range(0, SLOTS, 2 * C):
@@ -109,6 +116,8 @@ def tile_moe_shf_mlp_relu_kernel(
 
         w1_sb = [held([P, 2 * PASSES, 2 * H], U8, f"w1_sb{pair}") for pair in range(E // 2)]
         for pair in range(E // 2):
+            if pair % 2 == 0:
+                load_rows(w1_planes[pair // 2], w1_scales[2 * pair : 2 * pair + 4].rearrange("e s (q r) i -> r q (e s) i", r=4))
             if pair == 1:
                 for r in range(4):
                     nc.sync.dma_start(out=lifted[:].bitcast(I32)[r:P:32], in_=stacked[:].bitcast(I32)[4 + r : P : 32])
@@ -136,8 +145,6 @@ def tile_moe_shf_mlp_relu_kernel(
             for e in range(lo, lo + 2):
                 cols = slice((e - lo) * C, (e - lo + 1) * C)
                 picked[e] = [(words[s][:, cols], plane[:, e * C : (e + 1) * C]) for s, plane in enumerate((stacked, lifted))]
-
-        banks = [psum.tile([P, WIDTH], F32, name=f"bank{b}") for b in range(8)]
 
         shared_grouped = [[keep.tile([P, 2 * WIDTH], BF16, name=f"shared_grouped{g}_{pair}", tag=f"shared_grouped{g}_{pair}", align_bytes=64) for pair in range(2)] for g in range(SHARED_PASSES)]
         shared_codes = [keep.tile([P, T], U32, name=f"shared_codes{g}", tag=f"shared_codes{g}", align_bytes=64) for g in range(SHARED_PASSES)]
@@ -169,7 +176,7 @@ def tile_moe_shf_mlp_relu_kernel(
             for s in range(PASSES):
                 nc.tensor.matmul_mx(
                     out=bank[:], lhsT=picked[e][s][0].bitcast(FP8X4), lhsT_scale=picked[e][s][1],
-                    rhs=w1_sb[e // 2][:, e % 2 * PASSES + s, :].bitcast(FP4X4), rhs_scale=w1_plane[:, e * PASSES + s, :],
+                    rhs=w1_sb[e // 2][:, e % 2 * PASSES + s, :].bitcast(FP4X4), rhs_scale=w1_planes[e // 4][:, e % 4 * PASSES + s, :],
                     start=(s == 0), stop=(s == PASSES - 1),
                 )
             rounded = hiddens[e][:].bitcast(BF16).rearrange("s (u p e) -> s u p e", u=2, e=2)
@@ -213,14 +220,14 @@ def tile_moe_shf_mlp_relu_kernel(
         turn(0, banks[4], nc.vector.tensor_copy)
         for e in range(4, 6):
             routed_unit(e, banks[(e + EARLY) % 4])
-        turn(1, banks[5], nc.vector.tensor_copy)
+        turn(1, banks[0], nc.vector.tensor_copy)
         for e in range(6, 8):
             routed_unit(e, banks[(e + EARLY) % 4])
-        turn(2, banks[4], nc.vector.tensor_copy)
+        turn(2, banks[4], nc.scalar.copy)
         turn(3, banks[5], nc.vector.tensor_copy)
         turn(4, banks[0], nc.scalar.copy)
         second_layer(0, 0, 4, banks[6], nc.scalar.copy)
-        second_layer(0, 4, 7, banks[7], nc.vector.tensor_copy)
+        second_layer(0, 4, 7, banks[7], nc.scalar.copy)
         second_layer(0, 7, 8, banks[0], nc.vector.tensor_copy)
         second_layer(1, 0, 4, banks[4], nc.scalar.copy)
         second_layer(1, 4, 8, banks[5], nc.scalar.copy)
@@ -250,10 +257,13 @@ def tile_moe_shf_mlp_relu_kernel(
             nc.vector.tensor_tensor(terms[r][:], y_sb[0][:].indirect(token_lists[r][:]), gates[r][:], MULT)
         fetched = keep.tile([P, 2, T], F32, name="fetched", tag="w1s_sb1", align_bytes=64)
         columns = [fetched[:, r, :] for r in range(2)]
-        for r in range(2):
-            nc.scalar.activation(columns[r], y_sb[1][:].indirect(token_lists[r][:]), COPY)
+        other = held([P, T], F32, "other")
+        split = HALF // PER_COLUMN
+        nc.vector.tensor_tensor(other[:, :HALF], y_sb[1][:].indirect(token_lists[0][:, :split]), gates[0][:, :HALF], MULT)
+        nc.scalar.activation(columns[0][:, HALF:], y_sb[1][:].indirect(token_lists[0][:, split:]), COPY)
+        nc.scalar.activation(columns[1], y_sb[1][:].indirect(token_lists[1][:]), COPY)
         both = combined("both", terms[0][:], terms[1][:], ADD)
-        other = combined("other", columns[0], gates[0][:], MULT)
+        nc.vector.tensor_tensor(other[:, HALF:], columns[0][:, HALF:], gates[0][:, HALF:], MULT)
         total = combined("total", banks[1][:], both[:], ADD)
         nc.sync.dma_start(out=out_rows[:, 0, :], in_=total[:])
         part = combined("part", banks[2][:], other[:], ADD)

@@ -32,6 +32,7 @@ HALF = T // 2
 PER_COLUMN = 16
 GROUPS = [(0, 2), (2, 4), (4, 6), (6, 7), (7, 8)]
 EARLY = 4
+ON_VECTOR = 256
 WARM_UPS = 3
 W1S_FIRST = 4
 W2S_FIRST = 8
@@ -99,10 +100,10 @@ def tile_moe_shf_mlp_relu_kernel(
 
         def permute_plane(g):
             w1s_planes[g] = keep.tile([P, WIDTH], U8, name=f"w1s_plane{g}", tag="w1s_plane", align_bytes=64)
-            nc.gpsimd.tensor_copy(
-                out=w1s_planes[g][:].rearrange("p (t m) -> p t m", t=PACK),
-                in_=w1s_loaded_plane[:, g * WIDTH : (g + 1) * WIDTH].rearrange("p (m t) -> p t m", t=PACK),
-            )
+            permuted = w1s_planes[g][:].rearrange("p (t m) -> p t m", t=PACK)
+            loaded = w1s_loaded_plane[:, g * WIDTH : (g + 1) * WIDTH].rearrange("p (m t) -> p t m", t=PACK)
+            for lo in range(0, PACK, 2):
+                nc.gpsimd.tensor_copy(out=permuted[:, lo : lo + 2, :], in_=loaded[:, lo : lo + 2, :])
 
         def permute_words(g, copy):
             for s in range(PASSES):
@@ -258,19 +259,20 @@ def tile_moe_shf_mlp_relu_kernel(
         fetched = keep.tile([P, 2, T], F32, name="fetched", tag="w1s_sb1", align_bytes=64)
         columns = [fetched[:, r, :] for r in range(2)]
         other = held([P, T], F32, "other")
-        split = HALF // PER_COLUMN
-        nc.vector.tensor_tensor(other[:, :HALF], y_sb[1][:].indirect(token_lists[0][:, :split]), gates[0][:, :HALF], MULT)
-        nc.scalar.activation(columns[0][:, HALF:], y_sb[1][:].indirect(token_lists[0][:, split:]), COPY)
-        nc.scalar.activation(columns[1], y_sb[1][:].indirect(token_lists[1][:]), COPY)
+        split = ON_VECTOR // PER_COLUMN
+        nc.vector.tensor_tensor(other[:, :ON_VECTOR], y_sb[1][:].indirect(token_lists[0][:, :split]), gates[0][:, :ON_VECTOR], MULT)
+        nc.scalar.activation(columns[0][:, ON_VECTOR:], y_sb[1][:].indirect(token_lists[0][:, split:]), COPY)
+        for lo in (0, HALF):
+            nc.scalar.activation(columns[1][:, lo : lo + HALF], y_sb[1][:].indirect(token_lists[1][:, lo // PER_COLUMN : (lo + HALF) // PER_COLUMN]), COPY)
         both = combined("both", terms[0][:], terms[1][:], ADD)
-        nc.vector.tensor_tensor(other[:, HALF:], columns[0][:, HALF:], gates[0][:, HALF:], MULT)
+        nc.vector.tensor_tensor(other[:, ON_VECTOR:], columns[0][:, ON_VECTOR:], gates[0][:, ON_VECTOR:], MULT)
         total = combined("total", banks[1][:], both[:], ADD)
         nc.sync.dma_start(out=out_rows[:, 0, :], in_=total[:])
-        part = combined("part", banks[2][:], other[:], ADD)
         halves = [slice(half * HALF, (half + 1) * HALF) for half in range(2)]
-        last = keep.tile([P, T], F32, name="last", tag="shared_codes1", align_bytes=64)
+        parts = [combined(f"part{half}", banks[2][:, cols], other[:, cols], ADD) for half, cols in enumerate(halves)]
+        last = held([P, T], F32, "last")
         for cols in halves:
-            nc.vector.tensor_tensor(last[:, cols], columns[1][:, cols], gates[1][:, cols], MULT)
+            nc.gpsimd.tensor_tensor(last[:, cols], columns[1][:, cols], gates[1][:, cols], MULT)
         for half, cols in enumerate(halves):
-            total = combined(f"total{half}", part[:, cols], last[:, cols], ADD)
+            total = combined(f"total{half}", parts[half][:], last[:, cols], ADD)
             nc.sync.dma_start(out=out_rows[:, 1, cols], in_=total[:])

@@ -33,7 +33,6 @@ PER_COLUMN = 16
 GROUPS = [(0, 2), (2, 4), (4, 6), (6, 7), (7, 8)]
 EARLY = 4
 ON_VECTOR = 256
-WARM_UPS = 3
 W1S_FIRST = 4
 W2S_FIRST = 8
 
@@ -80,12 +79,6 @@ def tile_moe_shf_mlp_relu_kernel(
         w1s_rows = w1s_words.rearrange("s p l d -> p s (l d)").bitcast(I32)
         nc.sync.dma_start(out=w1s_loaded[0][:], in_=w1s_rows[:, :, :WIDTH])
         banks = [psum.tile([P, WIDTH], F32, name=f"bank{b}") for b in range(8)]
-        stand_in = w1s_loaded[0][:, 1, :].bitcast(U8)
-        for j in range(WARM_UPS):
-            nc.tensor.matmul_mx(
-                out=banks[7][:], lhsT=w1s_loaded[0][:, 0, :P].bitcast(FP8X4), lhsT_scale=stand_in[:, :P],
-                rhs=w1s_loaded[0][:, 0, :].bitcast(FP8X4), rhs_scale=stand_in[:, :WIDTH], start=True, stop=True,
-            )
         load_stacked(w1s_loaded_plane, w1s_scales, W1S_FIRST)
         x_sb = held([P, PASSES, T], I32, "x_sb")
         nc.sync.dma_start(out=x_sb[:], in_=x_words.rearrange("s p t d -> p s (t d)").bitcast(I32))

from contextlib import ExitStack

import concourse.mybir as mybir
from concourse.masks import make_identity

K, T, E, C, H, HS, N = 1024, 512, 8, 128, 512, 1024, 256
FLOPS = 2 * (T * (K * HS + HS * N) + E * C * (K * H + H * N))

F32 = mybir.dt.float32
BF16 = mybir.dt.bfloat16
I32 = mybir.dt.int32
U32 = mybir.dt.uint32
U16 = mybir.dt.uint16
U8 = mybir.dt.uint8
FP8X4 = mybir.dt.float8_e4m3fn_x4
FP4X4 = mybir.dt.float4_e2m1fn_x4
COPY = mybir.ActivationFunctionType.Copy
RELU = mybir.ActivationFunctionType.Relu
MULT = mybir.AluOpType.mult
ADD = mybir.AluOpType.add

P = 128
WIDTH = 512
WORDS = WIDTH // 2
PACK = 4
PASSES = K // WIDTH
SHARED_PASSES = HS // WIDTH
BLOCKS = N // P
SLOTS = E * C
TILES = T // P
HALF = T // 2
PER_COLUMN = 16
GROUPS = [(0, 2), (2, 4), (4, 6), (6, 7), (7, 8)]
EARLY = 4
ON_VECTOR = 256
W1S_FIRST = 4
W2S_FIRST = 8


def tile_moe_shf_mlp_relu_kernel(
    tc, x_words, x_scales, w1_words, w1_scales, w2_words, w2_scales, w1s_words, w1s_scales, w2s_words, w2s_scales, gate, offs, pos1, pos2, out
):
    nc = tc.nc
    with ExitStack() as ctx:
        keep = ctx.enter_context(tc.tile_pool(name="keep", bufs=1))
        psum = ctx.enter_context(tc.psum_pool(name="psum", bufs=1))

        def held(shape, dtype, name):
            return keep.tile(shape, dtype, name=name, align_bytes=64)

        def zeroed_plane(shape, name, engine):
            plane = held(shape, U8, name)
            engine.memset(plane[:].bitcast(I32), 0)
            return plane

        def load_rows(plane, rows):
            for r in range(4):
                nc.sync.dma_start(out=plane[:].bitcast(I32)[r:P:32], in_=rows[r].bitcast(I32))

        def load_stacked(plane, scales, first):
            for q in range(4):
                nc.sync.dma_start(
                    out=plane[:].bitcast(I32)[32 * q + first : 32 * q + first + 8], in_=scales[:, 4 * q : 4 * q + 4, :].bitcast(I32)
                )

        x_plane = zeroed_plane([P, T], "x_plane", nc.gpsimd)
        w1s_loaded_plane = zeroed_plane([P, HS], "w1s_loaded_plane", nc.gpsimd)
        w1_planes = [zeroed_plane([P, E // 2 * PASSES, H], f"w1_plane{half}", nc.vector) for half in range(2)]
        lifted = zeroed_plane([P, SLOTS], "lifted", nc.gpsimd)
        w2s_plane = zeroed_plane([P, N], "w2s_plane", nc.gpsimd)
        ident = held([P, P], F32, "ident")
        make_identity(nc, ident[:])
        w2_plane = zeroed_plane([P, E, N], "w2_plane", nc.gpsimd)

        slot_list = keep.tile([P, SLOTS // PER_COLUMN], U16, name="slot_list")
        nc.sync.dma_start(slot_list[:], offs)
        load_stacked(x_plane, x_scales, 0)
        w1s_loaded = [held([P, PASSES, WIDTH], I32, f"w1s_loaded{g}") for g in range(SHARED_PASSES)]
        w1s_rows = w1s_words.rearrange("s p l d -> p s (l d)").bitcast(I32)
        nc.sync.dma_start(out=w1s_loaded[0][:], in_=w1s_rows[:, :, :WIDTH])
        banks = [psum.tile([P, WIDTH], F32, name=f"bank{b}") for b in range(8)]
        load_stacked(w1s_loaded_plane, w1s_scales, W1S_FIRST)
        x_sb = held([P, PASSES, T], I32, "x_sb")
        nc.sync.dma_start(out=x_sb[:], in_=x_words.rearrange("s p t d -> p s (t d)").bitcast(I32))

        stacked = held([P, SLOTS], U8, "stacked")
        for lo in range(0, SLOTS, 2 * C):
            offsets = slot_list[:, lo // PER_COLUMN : (lo + 2 * C) // PER_COLUMN]
            nc.vector.tensor_copy(stacked[:, lo : lo + 2 * C], x_plane[:].indirect(offsets))

        w1s_sb = [keep.tile([P, PASSES, WIDTH], U32, name=f"w1s_sb{g}", tag=f"w1s_sb{g}", align_bytes=64) for g in range(SHARED_PASSES)]
        w1s_planes = {}

        def permute_plane(g):
            w1s_planes[g] = keep.tile([P, WIDTH], U8, name=f"w1s_plane{g}", tag="w1s_plane", align_bytes=64)
            permuted = w1s_planes[g][:].rearrange("p (t m) -> p t m", t=PACK)
            loaded = w1s_loaded_plane[:, g * WIDTH : (g + 1) * WIDTH].rearrange("p (m t) -> p t m", t=PACK)
            for lo in range(0, PACK, 2):
                nc.gpsimd.tensor_copy(out=permuted[:, lo : lo + 2, :], in_=loaded[:, lo : lo + 2, :])

        def permute_words(g, copy):
            for s in range(PASSES):
                copy(
                    out=w1s_sb[g][:, s, :].rearrange("p (t b i) -> p b t i", t=PACK, i=PACK),
                    in_=w1s_loaded[g][:, s, :].bitcast(U32).rearrange("p (b i t) -> p b t i", t=PACK, i=PACK),
                )

        permute_plane(0)
        permute_words(0, nc.scalar.copy)

        w1_sb = [held([P, 2 * PASSES, 2 * H], U8, f"w1_sb{pair}") for pair in range(E // 2)]
        for pair in range(E // 2):
            if pair % 2 == 0:
                load_rows(w1_planes[pair // 2], w1_scales[2 * pair : 2 * pair + 4].rearrange("e s (q r) i -> r q (e s) i", r=4))
            if pair == 1:
                for r in range(4):
                    nc.sync.dma_start(out=lifted[:].bitcast(I32)[r:P:32], in_=stacked[:].bitcast(I32)[4 + r : P : 32])
            experts = w1_words[2 * pair : 2 * pair + 2]
            nc.sync.dma_start(out=w1_sb[pair][:].bitcast(I32), in_=experts.rearrange("e s p b -> p (e s) b").bitcast(I32))
        nc.sync.dma_start(out=w1s_loaded[1][:], in_=w1s_rows[:, :, WIDTH:])
        load_rows(w2_plane, w2_scales.rearrange("e s (q r) n -> r q (e s) n", r=4))
        w2_sb = held([P, E, 2 * N], U8, "w2_sb")
        nc.sync.dma_start(out=w2_sb[:].bitcast(I32), in_=w2_words.rearrange("e s p b -> p (e s) b").bitcast(I32))
        token_lists = [keep.tile([P, T // PER_COLUMN], U16, name=f"token_list{r}") for r in range(2)]
        gates = [held([P, T], F32, f"gate{r}") for r in range(2)]
        for r, pos in enumerate((pos1, pos2)):
            nc.sync.dma_start(token_lists[r][:], pos)
            nc.sync.dma_start(out=gates[r][:], in_=gate[r])
        load_stacked(w2s_plane, w2s_scales, W2S_FIRST)
        w2s_sb = held([P, SHARED_PASSES, N], I32, "w2s_sb")
        nc.sync.dma_start(out=w2s_sb[:], in_=w2s_words.rearrange("s p n d -> p s (n d)").bitcast(I32))

        picked = {}
        for lo in range(0, E, 2):
            offsets = slot_list[:, lo * C // PER_COLUMN : (lo + 2) * C // PER_COLUMN]
            words = [held([P, 2 * C], U32, f"words{lo}_{s}") for s in range(PASSES)]
            for s in range(PASSES):
                nc.vector.tensor_copy(words[s][:], x_sb[:, s, :].bitcast(U32).indirect(offsets))
            for e in range(lo, lo + 2):
                cols = slice((e - lo) * C, (e - lo + 1) * C)
                picked[e] = [(words[s][:, cols], plane[:, e * C : (e + 1) * C]) for s, plane in enumerate((stacked, lifted))]

        shared_grouped = [[keep.tile([P, 2 * WIDTH], BF16, name=f"shared_grouped{g}_{pair}", tag=f"shared_grouped{g}_{pair}", align_bytes=64) for pair in range(2)] for g in range(SHARED_PASSES)]
        shared_codes = [keep.tile([P, T], U32, name=f"shared_codes{g}", tag=f"shared_codes{g}", align_bytes=64) for g in range(SHARED_PASSES)]
        shared_planes = [held([P, T], U8, f"shared_plane{g}") for g in range(SHARED_PASSES)]

        def shared_unit(g, tile, bank):
            cols = slice(tile * P, (tile + 1) * P)
            for t in range(PACK):
                features = slice(t * P, (t + 1) * P)
                for s in range(PASSES):
                    nc.tensor.matmul_mx(
                        out=bank[:, features],
                        lhsT=w1s_sb[g][:, s, features].bitcast(FP8X4), lhsT_scale=w1s_planes[g][W1S_FIRST + 4 * s :, features],
                        rhs=x_sb[:, s, cols].bitcast(FP8X4), rhs_scale=x_plane[4 * s :, cols], start=(s == 0), stop=(s == PASSES - 1),
                    )
            rounded = shared_grouped[g][tile // 2][:, tile % 2 * WIDTH : (tile % 2 + 1) * WIDTH]
            nc.scalar.activation(out=rounded.rearrange("p (k t) -> p k t", t=PACK), in_=bank[:].rearrange("p (t k) -> p k t", t=PACK), func=RELU)

        def quantise(codes, plane, grouped):
            nc.vector.quantize_mx(out=codes.bitcast(FP8X4), scales=plane, in_=grouped)

        def quantise_shared(g, pair):
            cols = slice(pair * HALF, (pair + 1) * HALF)
            quantise(shared_codes[g][:, cols], shared_planes[g][:, cols], shared_grouped[g][pair][:])

        hiddens = [held([P, WORDS], F32, f"h{e}") for e in range(E)]

        def routed_unit(e, bank):
            for s in range(PASSES):
                nc.tensor.matmul_mx(
                    out=bank[:], lhsT=picked[e][s][0].bitcast(FP8X4), lhsT_scale=picked[e][s][1],
                    rhs=w1_sb[e // 2][:, e % 2 * PASSES + s, :].bitcast(FP4X4), rhs_scale=w1_planes[e // 4][:, e % 4 * PASSES + s, :],
                    start=(s == 0), stop=(s == PASSES - 1),
                )
            rounded = hiddens[e][:].bitcast(BF16).rearrange("s (u p e) -> s u p e", u=2, e=2)
            nc.scalar.activation(out=rounded, in_=bank[:].rearrange("s (p u e) -> s u p e", u=2, e=2), func=RELU)

        routed = {}

        def turn(i, bank, copy):
            lo, hi = GROUPS[i]
            count = hi - lo
            turned = bank[:, : count * WORDS].rearrange("p (j u s) -> p j u s", j=count, u=2)
            for j in reversed(range(count)):
                for u in range(2):
                    nc.tensor.transpose(turned[:, j, u, :], hiddens[lo + j][:, u * P : (u + 1) * P], ident[:])
            grouped = held([P, count * WORDS], F32, f"grouped{i}")
            copy(out=grouped[:].rearrange("p (j s u) -> p j s u", j=count, u=2), in_=turned.rearrange("p j u s -> p j s u"))
            codes = held([P, count * C], U32, f"codes{i}")
            plane = held([P, count * C], U8, f"plane{i}")
            quantise(codes[:], plane[:], grouped[:].bitcast(BF16))
            for e in range(lo, hi):
                cols = slice((e - lo) * C, (e - lo + 1) * C)
                routed[e] = (codes[:, cols], plane[:, cols])

        y_sb = [held([P, SLOTS], F32, f"y_sb{b}") for b in range(BLOCKS)]

        def second_layer(b, lo, hi, results, copy):
            for e in range(lo, hi):
                nc.tensor.matmul_mx(
                    out=results[:, (e - lo) * C : (e - lo + 1) * C],
                    lhsT=w2_sb[:, e, 2 * b * P : 2 * (b + 1) * P].bitcast(FP4X4), lhsT_scale=w2_plane[:, e, b * P : (b + 1) * P],
                    rhs=routed[e][0].bitcast(FP8X4), rhs_scale=routed[e][1], start=True, stop=True,
                )
            copy(out=y_sb[b][:, lo * C : hi * C], in_=results[:, : (hi - lo) * C])

        for tile in range(EARLY):
            shared_unit(0, tile, banks[tile])
        for e in range(4):
            routed_unit(e, banks[(e + EARLY) % 4])
        quantise_shared(0, 0)
        quantise_shared(0, 1)
        turn(0, banks[4], nc.vector.tensor_copy)
        for e in range(4, 6):
            routed_unit(e, banks[(e + EARLY) % 4])
        turn(1, banks[0], nc.vector.tensor_copy)
        for e in range(6, 8):
            routed_unit(e, banks[(e + EARLY) % 4])
        turn(2, banks[4], nc.scalar.copy)
        turn(3, banks[5], nc.vector.tensor_copy)
        turn(4, banks[0], nc.scalar.copy)
        second_layer(0, 0, 4, banks[6], nc.scalar.copy)
        second_layer(0, 4, 7, banks[7], nc.scalar.copy)
        second_layer(0, 7, 8, banks[0], nc.vector.tensor_copy)
        second_layer(1, 0, 4, banks[4], nc.scalar.copy)
        second_layer(1, 4, 8, banks[5], nc.scalar.copy)
        permute_plane(1)
        permute_words(1, nc.vector.tensor_copy)
        for tile, bank in enumerate((6, 7, 0, 4)):
            shared_unit(1, tile, banks[bank])
            if tile % 2:
                quantise_shared(1, tile // 2)

        for g in range(SHARED_PASSES):
            for b, bank in enumerate((1, 2)):
                nc.tensor.matmul_mx(
                    out=banks[bank][:],
                    lhsT=w2s_sb[:, g, b * P : (b + 1) * P].bitcast(FP8X4), lhsT_scale=w2s_plane[W2S_FIRST + 4 * g :, b * P : (b + 1) * P],
                    rhs=shared_codes[g][:].bitcast(FP8X4), rhs_scale=shared_planes[g][:], start=(g == 0), stop=(g == SHARED_PASSES - 1),
                )

        def combined(name, left, right, op):
            result = held([P, right.shape[1]], F32, name)
            nc.vector.tensor_tensor(result[:], left, right, op)
            return result

        out_rows = out.rearrange("(b p) t -> p b t", p=P)
        terms = [held([P, T], F32, "term0"), held([P, T], F32, "term1")]
        for r in range(2):
            nc.vector.tensor_tensor(terms[r][:], y_sb[0][:].indirect(token_lists[r][:]), gates[r][:], MULT)
        fetched = keep.tile([P, 2, T], F32, name="fetched", tag="w1s_sb1", align_bytes=64)
        columns = [fetched[:, r, :] for r in range(2)]
        other = held([P, T], F32, "other")
        split = ON_VECTOR // PER_COLUMN
        nc.vector.tensor_tensor(other[:, :ON_VECTOR], y_sb[1][:].indirect(token_lists[0][:, :split]), gates[0][:, :ON_VECTOR], MULT)
        nc.scalar.activation(columns[0][:, ON_VECTOR:], y_sb[1][:].indirect(token_lists[0][:, split:]), COPY)
        for lo in (0, HALF):
            nc.scalar.activation(columns[1][:, lo : lo + HALF], y_sb[1][:].indirect(token_lists[1][:, lo // PER_COLUMN : (lo + HALF) // PER_COLUMN]), COPY)
        both = combined("both", terms[0][:], terms[1][:], ADD)
        nc.vector.tensor_tensor(other[:, ON_VECTOR:], columns[0][:, ON_VECTOR:], gates[0][:, ON_VECTOR:], MULT)
        total = combined("total", banks[1][:], both[:], ADD)
        nc.sync.dma_start(out=out_rows[:, 0, :], in_=total[:])
        halves = [slice(half * HALF, (half + 1) * HALF) for half in range(2)]
        parts = [combined(f"part{half}", banks[2][:, cols], other[:, cols], ADD) for half, cols in enumerate(halves)]
        last = held([P, T], F32, "last")
        for cols in halves:
            nc.gpsimd.tensor_tensor(last[:, cols], columns[1][:, cols], gates[1][:, cols], MULT)
        for half, cols in enumerate(halves):
            total = combined(f"total{half}", parts[half][:], last[:, cols], ADD)
            nc.sync.dma_start(out=out_rows[:, 1, cols], in_=total[:])
